import numpy as np, ml_dtypes
CORES = [3,11,19,27,35,43,51,59]
N = 8
BF = ml_dtypes.bfloat16
def gentries(a):
    return np.ascontiguousarray(a.reshape(8, 16, -1).transpose(0, 2, 1)).reshape(8, -1)
def gtable(e):
    e = np.asarray(e); return np.ascontiguousarray(e.reshape(8, -1, 16).transpose(0, 2, 1)).reshape(128, -1).astype(np.int32)
def f(rng, *shape):
    return (rng.standard_normal(shape, dtype=np.float32) * np.exp2(rng.integers(-2, 3, shape[:-1] + (1,)))).astype(BF)
def wide(rng, *shape):
    v = f(rng, *shape).astype(np.float32); k = shape[:-2] + (1, shape[-1])
    return (v * np.exp2(rng.integers(-6, 7, k)) * (rng.random(k) > 0.0625)).astype(BF)
V, H, M, RO, QN = 4096, 2048, 256, 3, 8
NO = V - 1
BIG = 2.0 ** 40
def grow(rng, par, lab, keep, nn, nm):
    B, q = nm.shape[0], nm.shape[2]; b = np.arange(B); C = np.full((B, M, 16), NO, np.int64)
    for i in range(M):
        up = C[b, par[:, i]]
        cand = np.concatenate([up, nm[:, i]], axis=1)
        use = np.concatenate([(rng.random((B, 16)) < keep[:, i, None]) & (up != NO), np.arange(q)[None, :] < nn[:, i, None]], axis=1)
        o = np.argsort(np.where(use, rng.random(use.shape), 2.0), axis=1)[:, :16]
        e = np.where(np.take_along_axis(use, o, 1), np.take_along_axis(cand, o, 1), NO)
        C[:, i] = np.take_along_axis(e, np.argsort(rng.random((B, 16)), axis=1), 1)
    D = np.empty_like(C); p = np.empty((B, M), np.int64)
    D[b[:, None], lab] = C; p[b[:, None], lab] = np.take_along_axis(lab, par, 1)
    return D, p
def fresh(rng):
    return np.argsort(rng.random((8 * N, V - 1)), axis=1)[:, :M * QN].reshape(8 * N, M, QN)
def shape(rng):
    B = 8 * N; n = np.arange(M)[None, :]; u = rng.random((B, M)); kind = rng.integers(0, 4, (B, 1))
    par = np.where(kind == 0, (u * n).astype(np.int64), np.where(kind == 1, n - 1 - (u * 8).astype(np.int64), np.where(kind == 2, (u * np.minimum(n, 12)).astype(np.int64), np.where(u > 0.7, n - 2, n - 1))))
    return np.maximum(par, 0), np.argsort(rng.random((B, M)), axis=1)
def trees(rng):
    par, lab = shape(rng); B = 8 * N
    keep = rng.choice(np.array([0.4, 0.7, 0.9, 1.0]), (B, M)); nn = np.where(rng.random((B, M)) < 0.15, 0, rng.integers(0, QN + 1, (B, M))); nn[:, 0] = QN
    return grow(rng, par, lab, keep, nn, fresh(rng))
def floats(rng):
    sc = np.exp2(rng.integers(-2, 3, (N, 128, 1))).astype(np.float32)
    x = (rng.standard_normal((N, 128, V), dtype=np.float32) * sc).astype(BF)
    col = np.repeat(1.5 * np.exp2(rng.integers(-3, 3, (N, 8, H))), 16, axis=1).astype(np.float32)
    return x, (np.abs(rng.standard_normal((N, 128, H), dtype=np.float32)) * sc * col).astype(BF)
def pack(x, l, C, p, th):
    C = C.reshape(N, 8, M * 16); p = p.reshape(N, 8, M)
    return {"xs": x, "lim": l, "cq": np.stack([gtable(a) for a in C]), "pt": np.stack([gtable(a) for a in p]), "th": np.asarray(th).astype(np.int32)}
def setup_inputs(rng):
    C, p = trees(rng); x, l = floats(rng)
    return pack(x, l, C, p, rng.integers(4, 17, (N, 8, 2)))
def setup_inputs_corners(rng):
    B = 8 * N; n = np.arange(M); par, lab = shape(rng); g = np.arange(B) & 7; k = (g + np.arange(B) // 8) & 7
    par[k < 2] = np.maximum(n - 1, 0); par[(k == 2) | (k == 3)] = 0; par[k == 4] = np.maximum(n - 1, 0) // 2
    lab[(k == 0) | (k == 2) | (k == 4)] = n; lab[(k == 1) | (k == 3)] = M - 1 - n
    mode = rng.integers(0, 6, (B, M)); mode[g == 5] = 2; mode[g == 6] = 3
    keep = np.array([0.0, 0.0, 1.0, 1.0, 0.93, 0.5])[mode]; nn = np.array([0, QN, 0, QN, 1, QN])[mode]; nn[:, 0] = QN; nn[g == 7, 0] = 0
    C, p = grow(rng, par, lab, keep, nn, fresh(rng)); x, l = floats(rng)
    th = rng.choice(np.array([0, 1, 8, 15, 16]), (N, 8, 2)); th[:, 0, 0] = 0; th[:, 1, 0] = 16; th[:, 5, 1] = 8
    return pack(x, l, C, p, th)
def setup_inputs_hubs(rng):
    B = 8 * N; n = np.arange(M); h = M // 2; k = ((np.arange(B) & 7) + np.arange(B) // 8) & 7
    hub = np.where(n > 1, 1, 0); star = np.zeros_like(n); teeth = np.where(n > h, n - h + 1, 0)
    low = n.copy(); low[0] = 1; low[1] = 0
    high = (n - 2) % M; swap = high.copy(); swap[0] = M - 1; swap[1] = M - 2
    comb = np.where(n > h, 2 * (n - h) - 1, 2 * (n - 1)); comb[0] = M - 1
    par = np.stack([hub, hub, hub, hub, star, star, hub, teeth])[k]; lab = np.stack([low, swap, low, high, M - 1 - n, n, low, comb])[k]
    mode = rng.integers(0, 6, (B, M))
    keep = np.array([0.0, 0.0, 1.0, 1.0, 0.93, 0.5])[mode]; nn = np.array([0, QN, 0, QN, 1, QN])[mode]
    a = (k == 0) | (k == 1); keep[a, 2:] = 0.0; keep[a, 1] = 1.0; nn[a, 1] = QN; keep[a, M - 1] = 1.0; nn[a, M - 1] = 0
    a = k == 6; keep[a, 2:] = np.where((n[2:] >= 3 * M // 4) & (rng.random((N, M - 2)) < 0.125), 0.5, 0.0); keep[a, 1] = 1.0; nn[a, 1] = QN
    a = (k == 2) | (k == 3); keep[a, 1] = 1.0; nn[a, 1] = 0
    a = (k == 4) | (k == 5); keep[a] = 1.0; nn[a] = 0
    a = k == 7; keep[a, 1:h + 1] = 1.0; nn[a, 1:h + 1] = 0
    nn[:, 0] = QN
    C, p = grow(rng, par, lab, keep, nn, fresh(rng)); x, l = floats(rng)
    th = np.stack([rng.choice(np.array([8, 12, 16]), (N, 8)), rng.choice(np.array([0, 8, 16]), (N, 8))], axis=2)
    return pack(x, l, C, p, th)
def setup_inputs_ends(rng):
    B = 8 * N; side = rng.integers(0, 2, (B, 1)); i = np.arange(V - 1)
    lab = np.concatenate([side * (M - 1), (1 - side) * (M - 1), 1 + np.argsort(rng.random((B, M - 2)), axis=1)], axis=1)
    par = rng.integers(0, 2, (B, M)); par[:, :2] = 0
    seq = np.where(i & 1 == 1, i // 2, V - 2 - i // 2); nm = np.full((B, M, QN), NO, np.int64)
    nm[:, 0] = seq[:QN]; nm[:, 1] = seq[QN:2 * QN]; nm[:, 2:, :2] = seq[2 * QN:2 * QN + 2 * (M - 2)].reshape(M - 2, 2)
    keep = np.full((B, M), 0.35); keep[:, 1] = 0.6; nn = rng.integers(0, 3, (B, M)); nn[:, :2] = QN
    C, p = grow(rng, par, lab, keep, nn, nm)
    for c in (0, M - 1):
        C[:, c] = np.sort(C[:, c], axis=1); C[3::4, c] = C[3::4, c, ::-1].copy()
    th = 16 * (np.argsort(rng.random((N, 8, 2)), axis=1) & 1)
    def signs(n, lows):
        kind = rng.integers(0, 2 + lows, (N, 8, 1, n)); kind[..., -2:] = 0
        s = np.where(kind == 0, 1, np.where(kind == 2, -1, 2 * rng.integers(0, 2, (N, 8, 16, n)) - 1))
        return (s * BIG).reshape(N, 128, n).astype(BF)
    return pack(signs(V, 0), signs(H, 1), C, p, th)
def setup_inputs_spread(rng):
    C, p = trees(rng); x = wide(rng, N, 128, V)
    l = np.abs(wide(rng, N, 128, H).astype(np.float32)) * np.where(rng.random((N, 1, H)) < 0.125, -1.0, 1.0)
    return pack(x, l.astype(BF), C, p, rng.integers(0, 17, (N, 8, 2)))
def setup_inputs_ties(rng):
    C, p = trees(rng)
    px = rng.choice(np.array([0.0, 0.75, 1.0, 256.0, -0.25, -1.5 * 2.0 ** -17]), (N, 8, 16, 6)); pl = rng.choice(np.array([0.0, 0.25, 1.0, 255.0, 256.0, 258.0, -1.0]), (N, 8, 16, 8))
    x = np.take_along_axis(px, rng.integers(0, 6, (N, 8, 1, V)), 3); l = np.take_along_axis(pl, rng.integers(0, 8, (N, 8, 1, H)), 3)
    return pack(x.reshape(N, 128, V).astype(BF), l.reshape(N, 128, H).astype(BF), C, p, rng.integers(5, 14, (N, 8, 2)))
def check_inputs(d):
    bad = []
    for k, hi in (("cq", NO), ("pt", M - 1), ("th", 16)):
        if np.min(d[k]) < 0 or np.max(d[k]) > hi: bad.append("range of " + k)
    for k in ("xs", "lim"):
        if not np.all(np.abs(np.asarray(d[k]).astype(np.float32)) <= BIG): bad.append("size of " + k)
    if "range of cq" in bad or "range of pt" in bad: return bad
    g = np.arange(8)[:, None]; own = np.arange(M)[None, :]
    for a in range(N):
        C = gentries(np.asarray(d["cq"][a])).astype(np.int64).reshape(8, M, 16); p = gentries(np.asarray(d["pt"][a])).astype(np.int64)
        e = np.sort(np.where(C == NO, -1 - np.arange(16), C), axis=2)
        if np.any(e[..., 1:] == e[..., :-1]) and "a name twice in a clique of cq" not in bad: bad.append("a name twice in a clique of cq")
        r = p
        for i in range(10): r = np.take_along_axis(r, r, 1)
        if (np.any(r != r[:, :1]) or np.any(np.take_along_axis(p, r, 1) != r)) and "pt not a tree" not in bad: bad.append("pt not a tree")
        inp = np.any(C[:, :, :, None] == C[g, p][:, :, None, :], axis=3)
        top = (C != NO) & (~inp | (p == own)[..., None])
        if np.max(np.bincount((C + V * np.arange(8)[:, None, None])[top], minlength=1)) > 1 and "cliques of a name not connected" not in bad: bad.append("cliques of a name not connected")
    return bad
def reference(xs, lim, cq, pt, th):
    C = np.stack([gentries(a) for a in cq]).astype(np.int64).reshape(N, 8, M, 16); P = np.stack([gentries(a) for a in pt]).astype(np.int64)
    X = xs.astype(np.float32).reshape(N, 8, 16, V); LM = lim.astype(np.float32).reshape(N, 8, 16, H); T = th.astype(np.int64)
    g = np.arange(8)[:, None]; own = np.arange(M)[None, :]; odd = [0] * N
    for t in range(RO):
        c = np.arange(t & 1, M, 2); m = len(c)
        for a in range(N):
            q = (a + t) % N; D = C[a]; pa = P[a]; full = D != NO
            up = D[g, pa]
            same = (D[:, :, :, None] == up[:, :, None, :]) & full[..., None]
            mark = np.any(same, axis=2) & (pa != own)[..., None]
            kids = np.zeros((8, M, 16), np.int64); np.add.at(kids, (g, pa), mark.astype(np.int64))
            e = D[:, c]; Q = up[:, c]; E = same[:, c]; pc = pa[:, c]; act = (pc & 1) != (t & 1)
            outside = full[:, c] & ~np.any(E, axis=3); has = np.any(outside, axis=2)
            y = np.where(has, np.take_along_axis(e, np.argmax(outside, axis=2)[..., None], 2)[..., 0], Q[..., 0])
            h = (((y[..., None] * Q) >> 5) + y[..., None] + 37 * Q) & (H - 1)
            XQ = np.take_along_axis(X[q], Q.reshape(8, 1, -1), 2).reshape(8, 16, m, 16)
            Xy = np.take_along_axis(X[q], y[:, None, :], 2)[..., None]
            LH = np.take_along_axis(LM[q], h.reshape(8, 1, -1), 2).reshape(8, 16, m, 16)
            s = np.add.reduce((np.abs(XQ - Xy) <= LH).astype(np.int64), axis=1)
            inC = np.any(E, axis=2); held = np.any(E & (kids[:, c] > 0)[..., None], axis=2); room = ~full[:, c]
            key = np.where((Q != NO) & ~inC, s, -1); j = np.argmax(key, axis=2); best = np.max(key, axis=2)
            join = act & has & (best >= 0) & (best >= T[q][:, :1] + odd[a]) & np.any(room, axis=2)
            can = inC & ~held; w = np.argmin(np.where(can, s, 17), axis=2)
            leave = act & has & ~join & np.any(can, axis=2); gone = act & ~has
            new = e.copy()
            i, n = np.nonzero(join); new[i, n, np.argmax(room[i, n], axis=1)] = Q[i, n, j[i, n]]
            i, n = np.nonzero(leave); new[i, n, np.argmax(E[i, n, :, w[i, n]], axis=1)] = NO
            i, n = np.nonzero(gone); new[i, n] = np.where(s[i, n] <= T[q][i, 1][:, None], Q[i, n], NO)
            A = np.broadcast_to(own, (8, M)).copy(); A[:, c] = np.where(gone, pc, c[None, :])
            D[:, c] = new; P[a] = np.take_along_axis(A, pa, 1); odd[a] = int(np.count_nonzero(join)) & 1
    return {"yc": np.stack([gtable(a.reshape(8, -1)) for a in C]).astype(np.float32), "yp": np.stack([gtable(a) for a in P]).astype(np.float32)}

@@ -1,0 +1,720 @@
+from concourse.bass import DstId, RemoteDMATransfer
+from concourse.mybir import dt, AluOpType, AxisListType, ActivationFunctionType
+
+V, H, M, NO = 4096, 2048, 256, 4095
+XW = V + H + 8
+NBF, NF32, NF16, NI32, NU16 = 36864, 10240, 2048, 2048, 1024
+SCRATCH = {
+    "XB0": ("sbuf", [128, XW], "bfloat16"), "XB1": ("sbuf", [128, XW], "bfloat16"), "XB2": ("sbuf", [128, XW], "bfloat16"),
+    "cqi": ("sbuf", [128, M], "int32"), "pti": ("sbuf", [128, 16], "int32"), "thi": ("sbuf", [128, 8], "int32"),
+    "Cf": ("sbuf", [128, M], "float32"), "Yc": ("sbuf", [128, M], "float32"), "ypo": ("sbuf", [128, 16], "float32"),
+    "bf": ("sbuf", [128, NBF], "bfloat16"), "f32": ("sbuf", [128, NF32], "float32"), "f16": ("sbuf", [128, NF16], "float16"),
+    "i32": ("sbuf", [128, NI32], "int32"), "u16": ("sbuf", [128, NU16], "uint16"),
+}
+for _b in range(8):
+    SCRATCH["ps%d" % _b] = ("psum", [128, 512], "float32")
+SEMAPHORES = ["sv", "sa", "sp", "sg", "lcq", "lpt", "lth", "oc", "op", "sent", "hx", "hl", "ax1", "al1", "ax2", "al2"] + \
+             ["lx%d" % k for k in range(4)] + ["ll%d" % k for k in range(4)]
+A = AluOpType
+F = ActivationFunctionType
+PAR = {"cy": 1.04, "pe": 0.5, "gam": 1.56, "ov": 40.0, "oa": 60.0, "same": 60.0, "cross": 120.0}
+CFG = {"bits": [1, 1, 1, 1, 1, 1], "diff": [0, 0, 0], "chunks": [512, 512, 512, 512], "up3": 0, "vc": [1, 1, 0], "wide": 3, "pen": 1000.0, "oh": 0, "iters": 1500, "seed": 3}
+PLAN = {}
+
+
+def pieces():
+    xs = [(1024 * k, 1024 * (k + 1)) for k in range(4)]
+    lm = [(V + 512 * k, V + 512 * (k + 1)) for k in range(4)]
+    lm[3] = (lm[3][0], XW)
+    return xs, lm
+
+
+def helpers_of(T, topo, r):
+    n = len(T.cores); me = T.cores[r]; d1 = T.cores[(r - 1) % n]
+    hs = [c for c in topo.cores_of(me) if c != me and T.rank_of(c) is None and topo.may_write(c, d1)]
+    hs.sort(key=lambda c: topo.die(c) == topo.die(me))
+    return hs[:3]
+
+
+def nbits(m):
+    return bin(m).count("1")
+
+
+def helper_program(g, core, T, topo):
+    n = len(T.cores)
+    for r in range(n):
+        hs = helpers_of(T, topo, r)
+        if core not in hs:
+            continue
+        k = hs.index(core); xs, lm = pieces(); me = T.cores[r]
+        inc = nbits(topo.mask(me, core) & ~topo.mask(me, T.cores[(r - 1) % n]))
+        tot = 0
+        for s in (1, 2):
+            dst = T.cores[(r - s) % n]; rid, pid, _ = topo.addr(dst); mk = topo.mask(core, dst)
+            for (a, b), hsem, asem in ((xs[k], "hx", "ax%d" % s), (lm[k], "hl", "al%d" % s)):
+                if s == 1:
+                    g.wait_ge(T.sem[hsem], inc)
+                g.remote_dma(T["XB%d" % s][:, a:b], T.XB0[:, a:b], T.sem[asem], T.sem.sent, pid, rid, mk)
+                tot += nbits(mk)
+        g.wait_ge(T.sem.sent, tot)
+
+
+def overlap(r, s):
+    if r[0] != s[0] or r[2] <= s[1] or s[2] <= r[1]:
+        return False
+    if r[3] == s[3] and r[3] > 1 and (r[1] - s[1]) % r[3] != 0:
+        return False
+    return True
+
+
+def build(T, topo, rank, place):
+    ops = []
+    nxt = {"bf": 0, "f32": 0, "f16": 0, "i32": 0, "u16": 0}
+    CY, PE, GAM, OV, OA = PAR["cy"], PAR["pe"], PAR["gam"], PAR["ov"], PAR["oa"]
+    temps = {}
+
+    def new(buf, n):
+        a = nxt[buf]; nxt[buf] = a + (n + 15) // 16 * 16
+        return (buf, a, a + n, 1)
+
+    def slot(n=128, whole=False):
+        name = "ps_%d" % len(temps); temps[name] = 4 if whole or n > 128 else 1
+        return (name, 0, n, 1)
+
+    def sub(r, a, b, st=1):
+        return (r[0], r[1] + a, r[1] + b, st)
+
+    def ap(r):
+        name, a, b = r[0], r[1], r[2]
+        if name in temps:
+            bank, c = place[name]; name = "ps%d" % bank; a += 128 * c; b += 128 * c
+        return T[name][:, a:b:r[3]] if r[3] > 1 else T[name][:, a:b]
+
+    def ln(r):
+        return (r[2] - r[1] + r[3] - 1) // r[3]
+
+    def two(*rs):
+        return all(r[0] in ("bf", "f16", "u16", "XB0", "XB1", "XB2") for r in rs)
+
+    def add(q, fn, rd, wr, cost, **kw):
+        o = {"alt": {q: (fn, cost)}, "rd": [r for r in rd if isinstance(r, tuple)], "wr": wr, "lat": 0.0}
+        o.update(kw); ops.append(o)
+
+    def val(x):
+        return ap(x) if isinstance(x, tuple) else x
+
+    def src(x):
+        return ap(x[0]).indirect(ap(x[1])) if isinstance(x, list) else ap(x)
+
+    def rds(x):
+        return list(x) if isinstance(x, list) else [x]
+
+    def vcost(out, x, per):
+        return 50 + ln(out) * GAM * CY if isinstance(x, list) else OV + max(64, ln(out) * per) * CY
+
+    def fast(out, x):
+        return 0.5 if not isinstance(x, list) and two(out, x) else 1
+
+    def cp(out, x):
+        add("v", lambda q: q.tensor_copy(ap(out), src(x)), rds(x), [out], vcost(out, x, fast(out, x)))
+
+    def ts(out, x, s1, o1, s2=None, o2=None):
+        def fn(q):
+            if o2 is None:
+                return q.tensor_scalar(ap(out), src(x), val(s1), None, o1)
+            return q.tensor_scalar(ap(out), src(x), val(s1), val(s2), o1, o2)
+        add("v", fn, rds(x) + [s1, s2], [out], vcost(out, x, fast(out, x)))
+
+    def tt(out, x, y, o):
+        per = 1 if (not isinstance(x, list) and x[0] in temps) or y[0] in temps else 2
+        add("v", lambda q: q.tensor_tensor(ap(out), src(x), ap(y), o), rds(x) + [y], [out], vcost(out, x, per))
+
+    def act(out, x, f, bias=0.0, scale=1.0, acc=None, extra=0.0, v=None):
+        def fn(q):
+            if acc is not None:
+                return q.activation(ap(out), src(x), f, bias=val(bias), scale=val(scale), accum_out=ap(acc))
+            return q.activation(ap(out), src(x), f, bias=val(bias), scale=val(scale))
+        c = 65 + ln(out) * GAM * CY if isinstance(x, list) else OA + max(64, ln(out)) * CY
+        add("a", fn, rds(x) + [bias, scale], [out] + ([acc] if acc else []), c + extra)
+        if v is not None:
+            o = ops.pop()
+            if v == ():
+                cp(out, x)
+            else:
+                ts(out, x, *v)
+            o["alt"]["v"] = ops[-1]["alt"]["v"]; o["rd"] = o["rd"] + ops[-1]["rd"]; ops[-1] = o
+
+    def lin(out, x, scale=1.0, bias=0.0):
+        act(out, x, F.Identity, bias=bias, scale=scale, v=() if (scale, bias) == (1.0, 0.0) else (scale, A.mult, bias, A.add))
+
+    def relu(out, x, bias=0.0):
+        act(out, x, F.Relu, bias=bias, v=(bias, A.add, 0.0, A.max))
+
+    def mm(groups, first=True, last=True):
+        def fn(q):
+            ins = None
+            for out, terms in groups:
+                for n, (l, r) in enumerate(terms):
+                    ins = q.matmul(ap(out), ap(l), ap(r), first and n == 0, last and n == len(terms) - 1)
+            return ins
+        rd = [x for _, terms in groups for t in terms for x in t]
+        c = sum(max(min(64, ln(l)), ln(r)) * (4 if l[0] == "f32" else 1) for _, terms in groups for l, r in terms)
+        add("p", fn, rd, [o for o, _ in groups], 30 + c * PE)
+
+    def mm1(terms, n=128):
+        p = slot(n); mm([(p, terms)])
+        return p
+
+    def dma(q, out, in_, rd, wr, sem, lat):
+        add(q, lambda e: e.dma_start(out, in_), rd, wr, 50.0, sem=sem, inc=16, lat=lat)
+
+    XB = [("XB%d" % t, 0, XW, 1) for t in range(3)]
+    Cf = ("Cf", 0, M, 1); cqi = ("cqi", 0, M, 1); pti = ("pti", 0, 16, 1); thi = ("thi", 0, 2, 1); ypo = ("ypo", 0, 16, 1)
+    Yc = ("Yc", 0, M, 1)
+    xsp, lmp = pieces()
+
+    dma("s", T.pti[:], T.pt[:], [], [pti], "lpt", 2000.0)
+    dma("s", T.cqi[:], T.cq[:], [], [cqi], "lcq", 2300.0)
+    dma("s", T.thi[0:8, 0:2], T.th[:], [], [thi], "lth", 2300.0)
+    for k, (a, b) in enumerate(xsp):
+        dma("s", T.XB0[:, a:b], T.xs[:, a:b], [], [sub(XB[0], a, b)], "lx%d" % k, 3200.0 + 900 * k)
+    for k, (a, b) in enumerate(lmp):
+        b = min(b, V + H)
+        dma("s", T.XB0[:, a:b], T.lim[:, a - V:b - V], [], [sub(XB[0], a, b)], "ll%d" % k, 6300.0 + 450 * k)
+    n = len(T.cores); me = T.cores[rank]
+    for s in (1, 2):
+        sender = T.cores[(rank + s) % n]
+        tot = sum(nbits(topo.mask(c, me)) for c in [sender] + helpers_of(T, topo, (rank + s) % n))
+        add("x", None, [], [sub(XB[s], 0, V)], 0.0, sem="ax%d" % s, inc=tot, lat=8000.0 + 10000 * s)
+        add("x", None, [], [sub(XB[s], V, XW)], 0.0, sem="al%d" % s, inc=tot, lat=11000.0 + 10000 * s)
+
+    def iota(out, pat, base, cm):
+        if out[0] == "i32":
+            add("g", lambda q: q.iota(ap(out), pat, base, cm), [], [out], 130 + 2 * ln(out) * CY)
+        else:
+            add("g", lambda q: q.iota(ap(out), pat, base, cm, allow_small_or_imprecise_dtypes=True), [], [out], 130 + 2 * ln(out) * CY)
+
+    def asel(out, x, pat, o, base, cm):
+        add("g", lambda q: q.affine_select(ap(out), ap(x), pat, o, 0.0, base, cm), [x], [out], 170 + 2 * ln(out) * CY)
+
+    def copy(out, x):
+        lin(out, x)
+        ops[-1]["alt"]["g"] = (lambda q: q.affine_select(ap(out), ap(x), [[0, ln(out)]], A.is_ge, 0.0, 0, 0), 170 + 2 * ln(out) * CY)
+
+    pI = new("i32", 1); iI = new("i32", 1); gI = new("i32", 1)
+    xh = new("bf", 128); iof = new("f32", M); ioP = new("bf", M); par = new("bf", M)
+    iota(pI, [[0, 1]], 0, 1)
+    iota(xh, [[1, 8], [0, 16]], 0, 0)
+    iota(iof, [[1, M]], 0, 0)
+    iota(ioP, [[1, 2], [2, 128]], 0, 0)
+    iota(par, [[0, 128], [1, 2]], 0, 0)
+    cP, cI, cG, cZ, cW, cS, cD, cU, cM = [new("f32", 1) for _ in range(9)]
+    eqk = new("f32", 16); nk0 = new("f32", 1); t16 = new("f32", 16); t16b = new("f32", 16)
+    ts(iI, pI, 15, A.bitwise_and); ts(gI, pI, 4, A.arith_shift_right)
+    cp(cP, pI); cp(cI, iI); cp(cG, gI)
+    ts(cZ, gI, 16.0, A.mult, 15.0, A.add)
+    B, nB, G8, I, nI, nIbig, I64, nI4k, I2k, B2080, I3232, nTri, Wr, Ba, Bb, Ua, Lb, nIh = [new("bf", 128) for _ in range(18)]
+    B32 = new("f32", 128); Z = new("bf", 143); Zw = new("bf", 143)
+    Sel = new("bf", 2048); S = new("bf", 2048); ones = new("bf", 512)
+    io128 = sub(iof, 0, 128); io16 = sub(iof, 0, 16); k0 = sub(eqk, 0, 1); one128 = sub(ones, 0, 128)
+    MAGIC = 12582912.0
+    ts(B, xh, cG, A.is_equal)
+    ts(eqk, io16, cI, A.is_equal)
+    ts(Z, sub(iof, 0, 143), cZ, A.is_equal)
+    ts(I, io128, cP, A.is_equal)
+    for k in range(16):
+        lin(sub(Sel, 128 * k, 128 * k + 128), B, scale=sub(eqk, k, k + 1))
+    ts(t16, io16, cI, A.is_lt, 1.0, A.add)
+    add("v", lambda q: q.tensor_reduce(ap(cW), ap(t16), AxisListType.X, A.mult), [t16], [cW], 110.0)
+    ts(t16b, io16, cI, A.is_gt, 1.0, A.add)
+    add("v", lambda q: q.tensor_reduce(ap(cS), ap(t16b), AxisListType.X, A.mult), [t16b], [cS], 110.0)
+    lin(Zw, Z, scale=cW)
+    if any(CFG["bits"]):
+        lin(cD, cS, scale=2.0 ** -16); lin(cU, cW, scale=2.0); lin(cM, cW, scale=-2.0 * MAGIC)
+    for o, x, s in ((nB, B, -1.0), (nI, I, -1.0), (I64, I, 2.0 ** -6), (nIbig, I, -65536.0), (nI4k, I, -4096.0), (I2k, I, 2048.0),
+                    (B2080, B, 2080.0), (I3232, I, 3232.0), (B32, B, 1.0), (Ba, B, 1.5), (Bb, B, 0.05), (nk0, k0, -1.0), (nIh, I, -0.5)):
+        lin(o, x, scale=s)
+    ts(G8, xh, cP, A.is_equal)
+    zero = new("bf", 256)
+    add("v", lambda q: q.memset(ap(zero), 0.0), [], [zero], OV + 128 * CY, early=1)
+    act(sub(ones, 0, 256), zero, F.Exp, extra=1600.0); ops[-1]["early"] = 1
+    copy(sub(ones, 256, 512), sub(ones, 0, 256))
+    asel(nTri, nB, [[1, 128]], A.is_gt, 0, -1)
+    for b in range(4):
+        asel(sub(S, 512 * b, 512 * b + 512), ones, [[1, 32], [0, 16]], A.is_equal, 32 * b, -1)
+    asel(Ua, Ba, [[1, 128]], A.is_gt, 0, -1); asel(Lb, Bb, [[-1, 128]], A.is_gt, 0, 1)
+    tt(Wr, Ua, Lb, A.add)
+    Gw = [new("bf", M), new("bf", M)]
+    for w in Gw:
+        iota(w, [[1, M]], 0, 0)
+    nI32 = new("f32", 128)
+    if 2 in CFG["bits"]:
+        lin(nI32, I, scale=-1.0)
+
+    def W(j, z=Z):
+        return sub(z, 15 - j, 143 - j)
+
+    thb = sub(zero, 0, 8)
+    add("v", lambda q: q.tensor_copy(T.bf[0:8, thb[1]:thb[1] + 2], T.thi[0:8, 0:2]), [thi, thb], [thb], 110.0)
+
+    ptu = new("u16", 16); Pn = new("bf", M)
+    cp(ptu, pti); ts(Cf, cqi, -2048.0, A.add)
+    lin(Pn, [iof, ptu])
+    L = [new("u16", 16) for _ in range(3)]; PS = [new("bf", M) for _ in range(4)]
+    for a in (0, 1):
+        p = mm1([(W(i), sub(Pn, 2 * i + a, M, 32)) for i in range(16)], 8)
+        ts(sub(L[0], 8 * a, 8 * a + 8), p, 0.0625, A.mult)
+        lin(sub(PS[0], 128 * a, 128 * a + 128), sub(Pn, a, M, 2))
+    lin(sub(XB[0], V + H, XW), mm1([(G8, thb)], 8))
+
+    nb = [0]; nr = [0]
+
+    def bits(out, x):
+        k = nb[0]; nb[0] += 1
+        if CFG["bits"][k]:
+            n1 = new("f32", 128); n2 = new("f32", 128)
+            p = mm1([(B, x), (I64, one128)])
+            act(n1, p, F.Identity, bias=MAGIC, scale=cD, v=(cD, A.mult, MAGIC, A.add))
+            act(n2, n1, F.Identity, bias=cM, scale=cU, v=(cU, A.mult, cM, A.add))
+            if CFG["bits"][k] == 1:
+                tt(out, p, n2, A.is_lt)
+            else:
+                act(out, mm1([(B, x), (I64, one128), (nI32, n2)]), F.Relu, scale=-1.0)
+                act(out, out, F.Sign, v=(0.0, A.is_gt))
+        else:
+            bI = new("i32", 128); bJ = new("i32", 128)
+            ts(bI, mm1([(B, x)]), cS, A.mult); ts(bJ, bI, 32768, A.bitwise_and); ts(out, bJ, 2.0 ** -15, A.mult)
+
+    def relation(a, Lst):
+        R = {k: new("bf", 128) for k in ("E", "Pm", "out", "fe", "inC", "inT")}
+        R["Dm"] = new("f16", 128); R["FC"] = new("f16", 128); R["xl"] = new("f16", 8)
+        eqb = new("bf", 2048); Ca = sub(Cf, a, M, 2); La = sub(Lst, 8 * a, 8 * a + 8)
+        relu(R["E"], Ca, -2046.0)
+        cp(R["Dm"], Ca)
+        diff = CFG["diff"][nr[0]]; nr[0] += 1
+        if diff:
+            uph = new("f16", 128); upe = new("bf", 128)
+            cp(uph, [Cf, La])
+            ts(upe, uph, 2047.0, A.is_equal)
+        else:
+            upr = new("f32", 512); u0 = new("f32", 128)
+            act(u0, [Cf, La], F.Relu, bias=2046.5, scale=-1.0, v=(2046.5, A.min, -1.0, A.mult))
+            u0v = ops[-1]
+            del u0v["alt"]["v"]
+            lin(sub(upr, 0, 128), u0, scale=-1.0, bias=2046.5)
+            for u in (1, 2, 3):
+                if CFG["up3"]:
+                    copy(sub(upr, 128 * u, 128 * u + 128), sub(upr, 0, 128))
+            if not CFG["up3"]:
+                copy(sub(upr, 128, 256), sub(upr, 0, 128))
+                copy(sub(upr, 256, 512), sub(upr, 0, 256))
+        Pk = slot(128, True)
+        for c in range(4):
+            bc = slot(512); eq = sub(eqb, 512 * c, 512 * c + 512)
+            more = [(nI, uph), (nI4k, upe)] if diff else []
+            mm([(sub(bc, 128 * u, 128 * u + 128), [(sub(Sel, 128 * (4 * c + u), 128 * (4 * c + u + 1)), R["Dm"])] + more) for u in range(4)])
+            if diff:
+                ts(eq, bc, 0.0, A.is_equal)
+            else:
+                tt(eq, bc, upr, A.is_equal)
+            terms = [(W(4 * c + u, Zw), sub(eq, 128 * u, 128 * u + 128)) for u in range(4)]
+            mm([(Pk, ([(I64, R["E"])] if c == 0 else []) + terms)], first=c == 0, last=c == 3)
+        act(R["out"], Pk, F.Relu, bias=1.0, scale=-64.0, v=(0.0, A.is_equal))
+        lin(R["Pm"], Pk)
+        first = mm1([(I, R["out"]), (nTri, R["out"])])
+        relu(first, first)
+        R["NH0"] = mm1([(B, R["out"])])
+        act(R["NH0"], R["NH0"], F.Relu, bias=k0, scale=nk0, v=(0.0, A.is_equal, k0, A.mult))
+        tt(R["FC"], first, R["Dm"], A.mult)
+        cp(R["xl"], mm1([(W(i), sub(R["FC"], i, 128, 16)) for i in range(16)], 8))
+        bits(R["inC"], R["Pm"])
+        relu(R["fe"], mm1([(I, R["E"]), (nTri, R["E"])]))
+        lin(R["inT"], mm1([(R["inC"], I)]))
+        return R
+
+    def acting(R, t):
+        a = t & 1
+        for k in ("act", "gone", "mJ0"):
+            R[k] = new("bf", 128)
+        R["Cn0"] = new("f32", 128); r0 = new("f32", 128)
+        lin(R["act"], [par, sub(L[t], 8 * a, 8 * a + 8)], scale=1.0 - 2 * a, bias=float(a))
+        relu(R["gone"], mm1([(I, R["act"]), (nB, R["out"])]))
+        p = mm1([(I, sub(PS[t], 128 * a, 128 * a + 128)), (nI, sub(ioP, 128 * a, 128 * a + 128))])
+        gd = new("bf", 128)
+        tt(gd, p, R["gone"], A.mult)
+        lin(sub(Gw[a], a, M, 2), mm1([(I, gd), (I, sub(ioP, 128 * a, 128 * a + 128))]))
+        lin(PS[t + 1], [Gw[a], L[t]])
+        if t < 2:
+            ts(L[t + 1], mm1([(W(i), sub(PS[t + 1], i, M, 16)) for i in range(16)], 16), 0.0625, A.mult)
+        else:
+            lin(ypo, mm1([(W(i), sub(PS[3], (i & 1) * 128 + (i >> 1), (i & 1) * 128 + 128, 8)) for i in range(16)], 16), scale=0.0625)
+            dma("s", T.yp[:], T.ypo[:], [ypo], [], "op", 2000.0)
+        relu(r0, mm1([(nI, R["Dm"]), (nI4k, R["gone"])]), 2047.0)
+        lin(R["Cn0"], r0, scale=-1.0, bias=4095.0 if t == 2 else 2047.0)
+
+    def onehots(t, lo, hi):
+        paT = new("f32", 16); w = hi - lo; OH = new("bf", 16 * w)
+        p = slot(16)
+        mm([(sub(p, 8 * ch, 8 * ch + 8), [(sub(PS[t], 128 * ch, 128 * ch + 128), sub(I, 0, 128, 16))]) for ch in (0, 1)])
+        lin(paT, p)
+        for u in range(16):
+            ts(sub(OH, w * u, w * u + w), sub(ioP, lo, hi), sub(paT, u, u + 1), A.is_equal)
+        return lambda ch, gr, a: sub(OH, w * (8 * ch + gr) + 128 * a - lo, w * (8 * ch + gr) + 128 * a - lo + 128)
+
+    def leaving(R, t, oh, marks):
+        a = t & 1
+        kb = new("bf", 128); Pc = new("bf", 128); can = new("bf", 128); R["can"] = can
+        p = slot()
+        mm([(sub(p, 16 * gr, 16 * gr + 16), [(oh(ch, gr, a), sub(marks[ch], 16 * gr, 16 * gr + 16)) for ch in (0, 1)]) for gr in range(8)])
+        lin(kb, p)
+        relu(Pc, mm1([(kb, nIbig), (I, R["Pm"])]))
+        bits(can, Pc)
+        R["sg"] = mm1([(I, can), (I, R["act"]), (nI, R["gone"])])
+        act(R["sg"], R["sg"], F.Sign, bias=1.5, scale=-1.0)
+
+    Qu = new("u16", 128); hu = new("u16", 128); ylu = new("u16", 8); Qh = new("f16", 128); rq = new("f16", 128)
+    pp = new("f32", 128); Qn = new("f32", 128); nI_ = new("i32", 128); hI = new("i32", 128)
+    Xy = new("bf", 128); XyT = new("bf", 128); XQ = new("bf", 2048); Cmp = new("bf", 2048); ad = new("f32", 2048)
+    odd = [None, new("i32", 1), new("i32", 1)]
+
+    def front(R, t):
+        a = t & 1; La = sub(L[t], 8 * a, 8 * a + 8); xw = sub(XB[t], 0, V); lw = sub(XB[t], V, V + H)
+        cp(Qh, [Cf, La])
+        ts(Qu, Qh, 2048.0, A.add)
+        tt(rq, R["NH0"], Qh, A.mult)
+        yl = mm1([(I, R["xl"])] + [(W(i), sub(rq, i, 128, 16)) for i in range(16)], 8)
+        y = mm1([(B, R["FC"]), (B, rq)])
+        lp = mm1([(B2080, R["FC"]), (B2080, rq), (I3232, Qh)])
+        tt(pp, y, Qh, A.mult)
+        tt(nI_, lp, pp, A.add)
+        ts(hI, nI_, 5, A.arith_shift_right, H - 1, A.bitwise_and)
+        cp(hu, hI)
+        ts(ylu, yl, 2048.0, A.add)
+        lin(Xy, [xw, ylu])
+        lin(XyT, mm1([(Xy, nI)]))
+        c0 = 0
+        for w in CFG["chunks"]:
+            c1 = c0 + w
+            lin(sub(XQ, c0, c1), [xw, sub(Qu, c0 // 16, c1 // 16)])
+            d = mm1([(I, sub(XQ, c0, c1)), (XyT, sub(S, c0, c1))], w)
+            act(sub(ad, c0, c1), d, F.Abs)
+            tt(sub(Cmp, c0, c1), [lw, sub(hu, c0 // 16, c1 // 16)], sub(ad, c0, c1), A.is_ge)
+            c0 = c1
+        lin(Qn, [Cf, La], scale=-1.0, bias=2047.0)
+
+    nfs, preJ, pre0, gg, tw, ws, mk, rw, nk, zb = [new("bf", 128) for _ in range(10)]
+    uu, QS, wq, Cn2, vc = [new("f32", 128) for _ in range(5)]
+
+    def decide(R, t):
+        a = t & 1
+        c1 = new("f32", 1); c2 = new("f32", 1); th1 = sub(XB[t], V + H, V + H + 1); th2 = sub(XB[t], V + H + 1, V + H + 2)
+        lin(c2, th2, scale=-1.0, bias=-20.0)
+        if t == 0:
+            lin(c1, th1, scale=-1.0, bias=40.0)
+        else:
+            c0 = new("f32", 1)
+            tt(c0, odd[t], th1, A.add)
+            lin(c1, c0, scale=-1.0, bias=40.0)
+        lin(pre0, R["gone"], scale=c2, bias=-40.0)
+        nc1 = new("f32", 1)
+        lin(nc1, c1, scale=-1.0)
+        act(nfs, Qn, F.Relu, bias=1.0, scale=-1.0, v=(0.0, A.is_equal))
+        act(preJ, mm1([(I, R["act"]), (nI, R["gone"]), (B, R["fe"]), (nI, R["inC"]), (nI, nfs)]), F.Relu, bias=nc1, scale=c1,
+            v=(1.5, A.is_gt, c1, A.mult))
+        tt(QS, R["sg"], Qn, A.mult)
+        z = slot(); vm = slot()
+        mlast = 128 - CFG["chunks"][-1] // 16
+        for m0, m1 in ((0, mlast), (mlast, 128)):
+            mm([(sub(z, m0, m1), [(I, sub(pre0, m0, m1)), (I, sub(preJ, m0, m1))] +
+                 [(W(j), sub(Cmp, 16 * m0 + j, 16 * m1, 16)) for j in range(16)])])
+        ts(gg, z, 0.0, A.is_ge, 41.0, A.mult)
+        tt(zb, z, gg, A.add)
+        tt(uu, R["sg"], zb, A.mult)
+        act(tw, uu, F.Exp, bias=-117.5, scale=3.4657359)
+        act(nk, zb, F.Sign, bias=59.5)
+        tt(Cn2, mm1([(I, Qh), (I2k, nk)] + [(I2k, one128)] * (2 if t == 2 else 1)), R["Cn0"], A.min)
+        Kp = mm1([(nI, R["Dm"]), (nI, R["fe"]), (I2k, one128)] if CFG["vc"][t] else [(I, R["Dm"]), (I, R["fe"])])
+        X = mm1([(Wr, tw)])
+        tt(X, X, tw, A.is_lt)
+        tt(wq, X, QS, A.mult)
+        v = mm1([(B32, wq)])
+        if CFG["vc"][t]:
+            act(vc, v, F.Relu, bias=1.0, scale=-1.0)
+        else:
+            ts(vc, v, 1.0, A.min, 2047.0, A.add)
+        tt(mk, Kp, vc, A.is_equal)
+        tt(vm, v, mk, A.mult)
+        tt(sub(Yc if t == 2 else Cf, a, M, 2), Cn2, vm, A.subtract)
+        if t == 2:
+            return None
+        act(ws, wq, F.Sign)
+        cT = new("bf", 128); jc = new("f32", 1); jb = new("bf", 1); oI = new("i32", 1)
+        relu(cT, mm1([(R["inC"], I), (R["can"], nIh), (R["gone"], nIh), (nk, nIh), (ws, I)]), 0.5)
+        act(rw, ws, F.Relu, acc=jc); lin(jb, jc)
+        cp(oI, mm1([(one128, jb)], 1)); ts(odd[t + 1], oI, 1, A.bitwise_and)
+        return cT
+
+    R0 = relation(0, L[0])
+    R1 = relation(1, L[0])
+    acting(R0, 0)
+    oh0 = onehots(0, 0, 128 if CFG["oh"] else 256)
+    leaving(R0, 0, oh0, [R0["inT"], R1["inT"]])
+    acting(R1, 1)
+    front(R0, 0)
+    cT0 = decide(R0, 0)
+    if CFG["oh"]:
+        oh0 = onehots(0, 128, 256)
+    leaving(R1, 1, oh0, [cT0, R1["inT"]])
+    R2 = relation(0, L[1])
+    acting(R2, 2)
+    oh1 = onehots(1, 0, 128)
+    front(R1, 1)
+    cT1 = decide(R1, 1)
+    lin(sub(Yc, 1, M, 2), sub(Cf, 1, M, 2), bias=2048.0)
+    leaving(R2, 2, oh1, [R2["inT"], cT1])
+    front(R2, 2)
+    decide(R2, 2)
+    dma("s", T.yc[:], T.Yc[:], [Yc], [], "oc", 2500.0)
+
+    hs = helpers_of(T, topo, rank); d1 = T.cores[(rank - 1) % n]
+
+    def send(dst, buf, a, b, sem, mask, due):
+        rid, pid, _ = topo.addr(dst)
+        add("g", lambda q: q.remote_dma(T[buf][:, a:b], T.XB0[:, a:b], T.sem[sem], T.sem.sent, pid, rid, mask),
+            [sub(XB[0], a, b), S, nTri], [], 500.0, remote=nbits(mask), lat=due)
+    for pc, hsem, asem in ((xsp, "hx", "ax1"), (lmp, "hl", "al1")):
+        for k, hc in enumerate(hs):
+            send(hc, "XB0", pc[k][0], pc[k][1], hsem, topo.mask(me, hc) & ~topo.mask(me, d1), 38000.0)
+        send(d1, "XB1", pc[3][0], pc[3][1], asem, topo.mask(me, d1), 38000.0)
+    d2 = T.cores[(rank - 2) % n]
+    for pc, asem in ((xsp, "ax2"), (lmp, "al2")):
+        send(d2, "XB2", pc[3][0], pc[3][1], asem, topo.mask(me, d2), 30000.0)
+    for k in nxt:
+        assert nxt[k] <= SCRATCH[k][1][1], (k, nxt[k])
+    return ops, temps
+
+
+def graph(ops, temps):
+    n = len(ops); deps = []; byname = {}
+    for i, o in enumerate(ops):
+        d = set()
+        for r in o["rd"] + o["wr"]:
+            for j, w, s in byname.get(r[0], []):
+                if w and overlap(r, s):
+                    d.add(j)
+        for r in o["wr"]:
+            for j, w, s in byname.get(r[0], []):
+                if overlap(r, s):
+                    d.add(j)
+        deps.append(d)
+        for r in o["rd"]:
+            byname.setdefault(r[0], []).append((i, False, r))
+        for r in o["wr"]:
+            byname.setdefault(r[0], []).append((i, True, r))
+    succ = [[] for _ in range(n)]
+    for i in range(n):
+        for j in deps[i]:
+            succ[j].append(i)
+    tmp = [sorted(set(r[0] for r in o["rd"] + o["wr"] if r[0] in temps)) for o in ops]
+    users = {t: [i for i in range(n) if t in tmp[i]] for t in temps}
+    return deps, succ, tmp, users
+
+
+def insert_schedule(ops, pred, succ, key, pen, back):
+    n = len(ops); same, cross = PAR["same"], PAR["cross"]
+    busy = {q: [] for q in "vapgsx"}; st = [0.0] * n; en = [0.0] * n; eng = [None] * n
+    left = [len(d) for d in pred]; ready = [i for i in range(n) if left[i] == 0]
+    while ready:
+        i = min(ready, key=lambda j: key[j]); ready.remove(i); best = None; o = ops[i]
+        for q in o["alt"]:
+            c = o["alt"][q][1]; t = o["lat"] if back and not pred[i] else 0.0
+            for j in pred[i]:
+                u = en[j] + (o["lat"] if back else ops[j]["lat"]) + (cross if eng[j] != q else 0.0 if q == "p" else same)
+                if u > t:
+                    t = u
+            for a, b in busy[q]:
+                if b <= t:
+                    continue
+                if a >= t + c:
+                    break
+                t = b
+            v = t + c + (pen[i] if q == "v" and len(o["alt"]) > 1 else 0.0)
+            if best is None or v < best[0]:
+                best = (v, q, t, c)
+        _, q, t, c = best
+        eng[i] = q; st[i] = t; en[i] = t + c; busy[q].append((t, t + c)); busy[q].sort()
+        for k in succ[i]:
+            left[k] -= 1
+            if left[k] == 0:
+                ready.append(k)
+    return st, en, eng
+
+
+def late_psum(ops, succ, st, en, eng):
+    row = sorted((i for i in range(len(ops)) if eng[i] == "p"), key=lambda i: -st[i]); placed = []
+    for i in row:
+        c = en[i] - st[i]
+        t = min([st[k] - (0.0 if eng[k] == "p" else PAR["cross"]) for k in succ[i]]) - c
+        for a, b in placed:
+            if a >= t + c:
+                continue
+            if b <= t:
+                break
+            t = a - c
+        if t > st[i]:
+            st[i] = t; en[i] = t + c
+        placed.append((st[i], en[i])); placed.sort(reverse=True)
+
+
+def realize(ops, temps, G, st, eng):
+    deps0, succ, tmp, users = G
+    n = len(ops); same, cross = PAR["same"], PAR["cross"]
+    for kind in ([i for i in range(n) if "remote" in ops[i]], [i for i in range(n) if eng[i] == "s" and not ops[i]["rd"]]):
+        for i, t in zip(kind, sorted(st[j] for j in kind)):
+            st[i] = t
+    seq = {q: sorted((i for i in range(n) if eng[i] == q), key=lambda i: (st[i], i)) for q in "vapgsx"}
+    deps = [set(d) for d in deps0]; end = [0.0] * n; start = [0.0] * n; left = [len(d) for d in deps0]; rt = [0.0] * n
+    free = dict.fromkeys(seq, 0.0); bank_by = [None] * 8; place = {}; order = []
+    tenant = [[None] * 4 for _ in range(8)]; todo = {t: len(users[t]) for t in temps}; gone_t = {}
+    while len(order) < n:
+        pick = None
+        for q in seq:
+            for i in seq[q][:8]:
+                if left[i]:
+                    break
+                t = max(free[q], rt[i]); where = None; ok = True
+                for x in tmp[i]:
+                    if x in place:
+                        u = bank_by[place[x][0]]
+                        if eng[u] != q and end[u] + cross > t:
+                            t = end[u] + cross
+                        continue
+                    best = None
+                    for b in range(8):
+                        u = bank_by[b]; tb = t if u is None or eng[u] == q else max(t, end[u] + cross)
+                        row = tenant[b]; live = sum(y is not None and todo[y] > 0 for y in row)
+                        if temps[x] == 4:
+                            if live:
+                                continue
+                            c = max([tb] + [gone_t[y] + cross for y in row if y is not None]); c = (c, b, 0, c)
+                        else:
+                            if live == 4 or b < CFG["wide"]:
+                                continue
+                            c = min((tb if y is None else max(tb, gone_t[y] + cross), s) for s, y in enumerate(row) if y is None or todo[y] == 0)
+                            c = (c[0] + 60 * live, b, c[1], c[0])
+                        if best is None or c[0] < best[0]:
+                            best = c
+                    if best is None:
+                        ok = False
+                        break
+                    t = best[3]; where = (x, best[1], best[2])
+                if ok:
+                    if pick is None or (t, st[i]) < pick[0]:
+                        pick = ((t, st[i]), i, where)
+                    break
+        if pick is None:
+            return None
+        (t, _), i, where = pick; q = eng[i]
+        start[i] = t; end[i] = t + ops[i]["alt"][q][1]; free[q] = end[i]; seq[q].remove(i); order.append(i)
+        if where:
+            x, b, s = where; place[x] = (b, s)
+            for c in range(s, s + temps[x]):
+                if tenant[b][c] is not None:
+                    deps[i].update(users[tenant[b][c]])
+                tenant[b][c] = x
+        for x in tmp[i]:
+            b = place[x][0]; u = bank_by[b]
+            if u is not None and u != i and eng[u] != q:
+                deps[i].add(u)
+            bank_by[b] = i; todo[x] -= 1
+            gone_t[x] = max(gone_t.get(x, 0.0), end[i])
+        for k in succ[i]:
+            rt[k] = max(rt[k], end[i] + ops[i]["lat"] + (cross if eng[k] != q else 0.0 if q == "p" else same)); left[k] -= 1
+    return max(end[i] + ops[i]["lat"] for i in range(n)), order, deps, place, start, eng
+
+
+def search(ops, temps, iters, seed):
+    G = graph(ops, temps); deps, succ = G[0], G[1]; n = len(ops); x = [seed]
+
+    def rnd(k):
+        x[0] = (x[0] * 1103515245 + 12345) % 2147483648
+        return (x[0] >> 8) % k
+    flex = [i for i in range(n) if len(ops[i]["alt"]) > 1]
+    tail = [0.0] * n
+    for i in range(n - 1, -1, -1):
+        tail[i] = min(a[1] for a in ops[i]["alt"].values()) + ops[i]["lat"] + max([PAR["cross"] + tail[k] for k in succ[i]] + [0.0])
+    key = [-t for t in tail]; pen = [CFG["pen"]] * n; best = None; cur = None
+    early = [i for i in range(n) if ops[i].get("early")]
+    for it in range(iters):
+        k2 = list(key); p2 = list(pen)
+        if it:
+            for _ in range(rnd(12)):
+                k2[rnd(n)] += (rnd(41) - 20) * 100.0
+            for _ in range(rnd(5)):
+                p2[flex[rnd(len(flex))]] = [5000.0, 2000.0, 1000.0, 500.0, 200.0, 0.0][rnd(6)]
+        for i in early:
+            k2[i] = -1e9
+        st, en, eng = insert_schedule(ops, deps, succ, k2, p2, False)
+        if it % 4 == 0:
+            sb, eb, _ = insert_schedule(ops, succ, deps, [-(en[i] + ops[i]["lat"]) for i in range(n)], p2, True)
+            k2 = [-e for e in eb]
+            for i in early:
+                k2[i] = -1e9
+            st, en, eng = insert_schedule(ops, deps, succ, k2, p2, False)
+        if cur is not None and max(en[i] + ops[i]["lat"] for i in range(n)) > cur + 400:
+            continue
+        late_psum(ops, succ, st, en, eng)
+        r = realize(ops, temps, G, st, eng)
+        if r is not None and (cur is None or r[0] <= cur + 300.0 * (1 - it / iters) * rnd(100) / 100):
+            cur = r[0]; key, pen = k2, p2
+            if best is None or r[0] < best[0]:
+                best = r
+    return best
+
+
+def rank_program(g, core, T, topo):
+    rank = T.rank_of(core)
+    if rank is None:
+        helper_program(g, core, T, topo)
+        return
+    place = {}
+    ops, temps = build(T, topo, rank, place)
+    if not PLAN:
+        PLAN["x"] = search(ops, temps, CFG["iters"], CFG["seed"])
+    _, order, deps, pl, _s, eng = PLAN["x"]
+    place.update(pl)
+    queue = {"v": g.vector, "a": g.scalar, "p": g.tensor, "g": g, "s": g.sync}
+    semof = {"v": "sv", "a": "sa", "p": "sp", "g": "sg"}
+    pos = {i: k for k, i in enumerate(order)}
+    need = set(); waits = {}
+    for i in order:
+        best = {}
+        for j in deps[i]:
+            if "sem" in ops[j] or eng[j] == "p" and eng[i] == "p":
+                continue
+            if eng[j] not in best or pos[j] > pos[best[eng[j]]]:
+                best[eng[j]] = j
+        waits[i] = list(best.values()) + sorted(j for j in deps[i] if "sem" in ops[j])
+        need.update(best.values())
+    count = {}; waited = {}; sent = 0; tok = {}
+    for i in order:
+        o = ops[i]; q = eng[i]
+        if q == "x":
+            tok[i] = (o["sem"], o["inc"]); count[o["sem"]] = o["inc"]
+            continue
+        for j in waits[i]:
+            s, c = tok[j]
+            if waited.get((q, s), 0) < c:
+                queue[q].wait_ge(T.sem[s], c); waited[(q, s)] = c
+        ins = o["alt"][q][0](queue[q])
+        if "remote" in o:
+            sent += o["remote"]
+        elif "sem" in o:
+            ins.then_inc(T.sem[o["sem"]], 16); tok[i] = (o["sem"], 16); count[o["sem"]] = 16
+        elif i in need:
+            s = semof[q]; count[s] = count.get(s, 0) + 1
+            ins.then_inc(T.sem[s], 1); tok[i] = (s, count[s])
+    g.wait_ge(T.sem.sent, sent)
+    for s in count:
+        if max([c for (q, s2), c in waited.items() if s2 == s] + [0]) < count[s]:
+            g.sync.wait_ge(T.sem[s], count[s])

@@ -2,60 +2,102 @@ from concourse.bass import DstId, RemoteDMATransfer
 from concourse.mybir import dt, AluOpType, AxisListType, ActivationFunctionType
 
 V, H, M, NO = 4096, 2048, 256, 4095
-XW = V + H + 8
+TO, XO = H, H + 16
+QO = XO + V
+XW = QO + 2048
 NBF, NF32, NF16, NI32, NU16 = 36864, 10240, 2048, 2048, 1024
 SCRATCH = {
     "XB0": ("sbuf", [128, XW], "bfloat16"), "XB1": ("sbuf", [128, XW], "bfloat16"), "XB2": ("sbuf", [128, XW], "bfloat16"),
     "cqi": ("sbuf", [128, M], "int32"), "pti": ("sbuf", [128, 16], "int32"), "thi": ("sbuf", [128, 8], "int32"),
-    "Cf": ("sbuf", [128, M], "float32"), "Yc": ("sbuf", [128, M], "float32"), "ypo": ("sbuf", [128, 16], "float32"),
+    "Ct": ("sbuf", [128, M], "float32"), "Yc": ("sbuf", [128, M], "float32"), "ypo": ("sbuf", [128, 16], "float32"),
     "bf": ("sbuf", [128, NBF], "bfloat16"), "f32": ("sbuf", [128, NF32], "float32"), "f16": ("sbuf", [128, NF16], "float16"),
     "i32": ("sbuf", [128, NI32], "int32"), "u16": ("sbuf", [128, NU16], "uint16"),
 }
 for _b in range(8):
     SCRATCH["ps%d" % _b] = ("psum", [128, 512], "float32")
-SEMAPHORES = ["sv", "sa", "sp", "sg", "lcq", "lpt", "lth", "oc", "op", "sent", "hx", "hl", "ax1", "al1", "ax2", "al2"] + \
+SEMAPHORES = ["sv", "sa", "sp", "sg", "lcq", "lpt", "lth", "oc", "op", "sent", "hx", "hl", "ax1", "al1", "ax2", "al2", "af"] + \
              ["lx%d" % k for k in range(4)] + ["ll%d" % k for k in range(4)]
 A = AluOpType
 F = ActivationFunctionType
-PAR = {"cy": 1.04, "pe": 0.5, "gam": 1.56, "ov": 40.0, "oa": 60.0, "same": 60.0, "cross": 120.0}
-CFG = {"bits": [1, 1, 1, 1, 1, 1], "diff": [0, 0, 0], "chunks": [512, 512, 512, 512], "up3": 0, "vc": [1, 1, 0], "wide": 3, "pen": 1000.0, "oh": 0, "iters": 1500, "seed": 3}
+PAR = {"cy": 1.04, "pe": 0.5, "gam": 1.56, "ov": 40.0, "oa": 60.0, "same": 60.0, "cross": 120.0, "net": [5000.0, 10000.0, 5000.0, 10000.0], "rc": 500.0}
+CFG = {"relay": 1, "full": 1, "soon": 0.05, "eqw": [512, 512, 512], "inc": [0, 0, 0], "oh": 0, "xqv": [[], [3], [3]], "zcut": [[0, 64, 128]] * 3, "chunks": [[512, 512, 512, 512]] * 3, "wide": 3, "pen": 1000.0, "iters": 400, "seed": 3,
+       "moves": 25000, "temp": 100.0, "mean": 0.2}
 PLAN = {}
+S0 = 12288.0
 
 
 def pieces():
-    xs = [(1024 * k, 1024 * (k + 1)) for k in range(4)]
-    lm = [(V + 512 * k, V + 512 * (k + 1)) for k in range(4)]
-    lm[3] = (lm[3][0], XW)
+    xs = [(XO + 1024 * k, XO + 1024 * (k + 1)) for k in range(4)]
+    lm = [(512 * k, 512 * (k + 1)) for k in range(4)]
+    lm[3] = (lm[3][0], XO)
     return xs, lm
-
-
-def helpers_of(T, topo, r):
-    n = len(T.cores); me = T.cores[r]; d1 = T.cores[(r - 1) % n]
-    hs = [c for c in topo.cores_of(me) if c != me and T.rank_of(c) is None and topo.may_write(c, d1)]
-    hs.sort(key=lambda c: topo.die(c) == topo.die(me))
-    return hs[:3]
 
 
 def nbits(m):
     return bin(m).count("1")
 
 
-def helper_program(g, core, T, topo):
-    n = len(T.cores)
+def routes(T, topo):
+    n = len(T.cores); xs, lm = pieces(); out = {}
+
+    def sides(r, dst):
+        me = T.cores[r]; cs = sorted(topo.cores_of(me), key=lambda c: (topo.die(c) == topo.die(me), c == me))
+        return [c for c in cs if topo.may_write(c, dst)], [c for c in cs if not topo.may_write(c, dst)]
+
+    def put(c, sbuf, pc, wait, dst, dbuf, sem, mask=None):
+        out.setdefault(c, []).append((sbuf, pc, wait, dst, dbuf, sem, topo.mask(c, dst) if mask is None else mask))
+
+    late = []
     for r in range(n):
-        hs = helpers_of(T, topo, r)
-        if core not in hs:
-            continue
-        k = hs.index(core); xs, lm = pieces(); me = T.cores[r]
-        inc = nbits(topo.mask(me, core) & ~topo.mask(me, T.cores[(r - 1) % n]))
-        tot = 0
-        for s in (1, 2):
-            dst = T.cores[(r - s) % n]; rid, pid, _ = topo.addr(dst); mk = topo.mask(core, dst)
-            for (a, b), hsem, asem in ((xs[k], "hx", "ax%d" % s), (lm[k], "hl", "al%d" % s)):
-                if s == 1:
-                    g.wait_ge(T.sem[hsem], inc)
-                g.remote_dma(T["XB%d" % s][:, a:b], T.XB0[:, a:b], T.sem[asem], T.sem.sent, pid, rid, mk)
-                tot += nbits(mk)
+        me, d1, d2 = T.cores[r], T.cores[(r - 1) % n], T.cores[(r - 2) % n]
+        P, O = sides(r, d1); home = topo.mask(me, P[0]) & ~topo.mask(me, d1)
+        relay = CFG["relay"] and not topo.mates(topo.chip(me), topo.chip(d1)) and topo.mates(topo.chip(d1), topo.chip(d2))
+        for k in range(3):
+            put(me, "XB0", xs[k], None, P[k], "XB0", "hx", None if CFG["full"] else home)
+            put(P[k], "XB0", xs[k], "hx", d1, "XB1", "ax1")
+        put(me, "XB0", xs[3], None, d1, "XB1", "ax1")
+        if relay:
+            P2 = sides((r - 2) % n, d1)[0]
+            for k in range(4):
+                put(me, "XB0", lm[k], None, O[k], "XB0", "hl", home)
+                put(O[k], "XB0", lm[k], "hl", P2[k], "XB2", "af")
+                late.append((P2[k], "XB2", lm[k], "af", d1, "XB1", "al1"))
+                if k < 3:
+                    put(P[k], "XB0", xs[k], None, O[k], "XB0", "hx", home)
+                    put(O[k], "XB0", xs[k], "hx", d2, "XB2", "ax2")
+                    late.append((P2[k], "XB2", lm[k], None, d2, "XB2", "al2", home))
+            late.append((me, "XB0", xs[3], None, d2, "XB2", "ax2"))
+        else:
+            for k in range(3):
+                put(me, "XB0", lm[k], None, P[k], "XB0", "hl", home)
+                put(P[k], "XB0", lm[k], "hl", d1, "XB1", "al1")
+                put(P[k], "XB0", xs[k], None, d2, "XB2", "ax2")
+                put(P[k], "XB0", lm[k], None, d2, "XB2", "al2")
+            put(me, "XB0", lm[3], None, d1, "XB1", "al1")
+            put(me, "XB0", lm[3], None, d2, "XB2", "af")
+            put(me, "XB0", xs[3], None, d2, "XB2", "ax2")
+    for w in sorted(late, key=lambda w: w[5] == "XB2"):
+        put(*w)
+    return out
+
+
+def arrivals(R, core):
+    got = {}
+    for ws in R.values():
+        for w in ws:
+            if w[3] == core:
+                got[w[5]] = got.get(w[5], 0) + nbits(w[6])
+    return got
+
+
+def helper_program(g, core, T, topo):
+    R = routes(T, topo); got = arrivals(R, core); tot = 0
+    for sbuf, (a, b), wait, dst, dbuf, sem, mask in R.get(core, []):
+        if wait:
+            g.wait_ge(T.sem[wait], got[wait])
+        rid, pid, _ = topo.addr(dst)
+        g.remote_dma(T[dbuf][:, a:b], T[sbuf][:, a:b], T.sem[sem], T.sem.sent, pid, rid, mask); tot += nbits(mask)
+    if tot:
         g.wait_ge(T.sem.sent, tot)
 
 
@@ -100,6 +142,21 @@ def build(T, topo, rank, place):
         o = {"alt": {q: (fn, cost)}, "rd": [r for r in rd if isinstance(r, tuple)], "wr": wr, "lat": 0.0}
         o.update(kw); ops.append(o)
 
+    def either(*makers):
+        o = None
+        for mk in makers:
+            mk(); x = ops.pop()
+            if o is None:
+                o = x
+            else:
+                o["alt"].update(x["alt"]); o["rd"] = o["rd"] + x["rd"]
+        ops.append(o)
+
+    def row(name, k, q=None):
+        ops[-1].setdefault("row", []).append((name, k))
+        if q:
+            ops[-1]["alt"] = {q: ops[-1]["alt"][q]}
+
     def val(x):
         return ap(x) if isinstance(x, tuple) else x
 
@@ -129,26 +186,20 @@ def build(T, topo, rank, place):
         per = 1 if (not isinstance(x, list) and x[0] in temps) or y[0] in temps else 2
         add("v", lambda q: q.tensor_tensor(ap(out), src(x), ap(y), o), rds(x) + [y], [out], vcost(out, x, per))
 
-    def act(out, x, f, bias=0.0, scale=1.0, acc=None, extra=0.0, v=None):
-        def fn(q):
-            if acc is not None:
-                return q.activation(ap(out), src(x), f, bias=val(bias), scale=val(scale), accum_out=ap(acc))
-            return q.activation(ap(out), src(x), f, bias=val(bias), scale=val(scale))
+    def act(out, x, f, bias=0.0, scale=1.0, extra=0.0):
         c = 65 + ln(out) * GAM * CY if isinstance(x, list) else OA + max(64, ln(out)) * CY
-        add("a", fn, rds(x) + [bias, scale], [out] + ([acc] if acc else []), c + extra)
-        if v is not None:
-            o = ops.pop()
-            if v == ():
-                cp(out, x)
-            else:
-                ts(out, x, *v)
-            o["alt"]["v"] = ops[-1]["alt"]["v"]; o["rd"] = o["rd"] + ops[-1]["rd"]; ops[-1] = o
+        add("a", lambda q: q.activation(ap(out), src(x), f, bias=val(bias), scale=val(scale)), rds(x) + [bias, scale], [out], c + extra)
 
     def lin(out, x, scale=1.0, bias=0.0):
-        act(out, x, F.Identity, bias=bias, scale=scale, v=() if (scale, bias) == (1.0, 0.0) else (scale, A.mult, bias, A.add))
+        either(lambda: act(out, x, F.Identity, bias=bias, scale=scale),
+               lambda: cp(out, x) if (scale, bias) == (1.0, 0.0) else ts(out, x, scale, A.mult, bias, A.add))
 
-    def relu(out, x, bias=0.0):
-        act(out, x, F.Relu, bias=bias, v=(bias, A.add, 0.0, A.max))
+    def relu(out, x, bias=0.0, scale=1.0):
+        either(lambda: act(out, x, F.Relu, bias=bias, scale=scale),
+               lambda: ts(out, x, bias, A.add, 0.0, A.max) if scale == 1.0 else ts(out, x, scale, A.mult, 0.0, A.max))
+
+    def pcost(l, r):
+        return max(min(64, ln(l)), ln(r)) * (4 if l[0] == "f32" else 1)
 
     def mm(groups, first=True, last=True):
         def fn(q):
@@ -158,8 +209,7 @@ def build(T, topo, rank, place):
                     ins = q.matmul(ap(out), ap(l), ap(r), first and n == 0, last and n == len(terms) - 1)
             return ins
         rd = [x for _, terms in groups for t in terms for x in t]
-        c = sum(max(min(64, ln(l)), ln(r)) * (4 if l[0] == "f32" else 1) for _, terms in groups for l, r in terms)
-        add("p", fn, rd, [o for o, _ in groups], 30 + c * PE)
+        add("p", fn, rd, [o for o, _ in groups], 30 + PE * sum(pcost(l, r) for _, terms in groups for l, r in terms))
 
     def mm1(terms, n=128):
         p = slot(n); mm([(p, terms)])
@@ -169,326 +219,319 @@ def build(T, topo, rank, place):
         add(q, lambda e: e.dma_start(out, in_), rd, wr, 50.0, sem=sem, inc=16, lat=lat)
 
     XB = [("XB%d" % t, 0, XW, 1) for t in range(3)]
-    Cf = ("Cf", 0, M, 1); cqi = ("cqi", 0, M, 1); pti = ("pti", 0, 16, 1); thi = ("thi", 0, 2, 1); ypo = ("ypo", 0, 16, 1)
+    Ct = ("Ct", 0, M, 1); cqi = ("cqi", 0, M, 1); pti = ("pti", 0, 16, 1); thi = ("thi", 0, 2, 1); ypo = ("ypo", 0, 16, 1)
     Yc = ("Yc", 0, M, 1)
     xsp, lmp = pieces()
+
+    def half(r, a):
+        return sub(r, 128 * a, 128 * a + 128)
 
     dma("s", T.pti[:], T.pt[:], [], [pti], "lpt", 2000.0)
     dma("s", T.cqi[:], T.cq[:], [], [cqi], "lcq", 2300.0)
     dma("s", T.thi[0:8, 0:2], T.th[:], [], [thi], "lth", 2300.0)
     for k, (a, b) in enumerate(xsp):
-        dma("s", T.XB0[:, a:b], T.xs[:, a:b], [], [sub(XB[0], a, b)], "lx%d" % k, 3200.0 + 900 * k)
+        dma("s", T.XB0[:, a:b], T.xs[:, a - XO:b - XO], [], [sub(XB[0], a, b)], "lx%d" % k, 3200.0 + 900 * k)
     for k, (a, b) in enumerate(lmp):
-        b = min(b, V + H)
-        dma("s", T.XB0[:, a:b], T.lim[:, a - V:b - V], [], [sub(XB[0], a, b)], "ll%d" % k, 6300.0 + 450 * k)
-    n = len(T.cores); me = T.cores[rank]
-    for s in (1, 2):
-        sender = T.cores[(rank + s) % n]
-        tot = sum(nbits(topo.mask(c, me)) for c in [sender] + helpers_of(T, topo, (rank + s) % n))
-        add("x", None, [], [sub(XB[s], 0, V)], 0.0, sem="ax%d" % s, inc=tot, lat=8000.0 + 10000 * s)
-        add("x", None, [], [sub(XB[s], V, XW)], 0.0, sem="al%d" % s, inc=tot, lat=11000.0 + 10000 * s)
+        b = min(b, H)
+        dma("s", T.XB0[:, a:b], T.lim[:, a:b], [], [sub(XB[0], a, b)], "ll%d" % k, 6300.0 + 450 * k)
 
     def iota(out, pat, base, cm):
-        if out[0] == "i32":
-            add("g", lambda q: q.iota(ap(out), pat, base, cm), [], [out], 130 + 2 * ln(out) * CY)
-        else:
-            add("g", lambda q: q.iota(ap(out), pat, base, cm, allow_small_or_imprecise_dtypes=True), [], [out], 130 + 2 * ln(out) * CY)
+        add("g", lambda q: q.iota(ap(out), pat, base, cm, allow_small_or_imprecise_dtypes=True), [], [out], 130 + 2 * ln(out) * CY)
 
-    def asel(out, x, pat, o, base, cm):
-        add("g", lambda q: q.affine_select(ap(out), ap(x), pat, o, 0.0, base, cm), [x], [out], 170 + 2 * ln(out) * CY)
+    def asel(out, x, pat, o, base, cm, fill=0.0):
+        add("g", lambda q: q.affine_select(ap(out), ap(x), pat, o, fill, base, cm), [x], [out], 170 + 2 * ln(out) * CY)
 
     def copy(out, x):
-        lin(out, x)
-        ops[-1]["alt"]["g"] = (lambda q: q.affine_select(ap(out), ap(x), [[0, ln(out)]], A.is_ge, 0.0, 0, 0), 170 + 2 * ln(out) * CY)
+        either(lambda: lin(out, x), lambda: asel(out, x, [[0, ln(out)]], A.is_ge, 0, 0))
 
-    pI = new("i32", 1); iI = new("i32", 1); gI = new("i32", 1)
-    xh = new("bf", 128); iof = new("f32", M); ioP = new("bf", M); par = new("bf", M)
-    iota(pI, [[0, 1]], 0, 1)
-    iota(xh, [[1, 8], [0, 16]], 0, 0)
-    iota(iof, [[1, M]], 0, 0)
-    iota(ioP, [[1, 2], [2, 128]], 0, 0)
-    iota(par, [[0, 128], [1, 2]], 0, 0)
-    cP, cI, cG, cZ, cW, cS, cD, cU, cM = [new("f32", 1) for _ in range(9)]
-    eqk = new("f32", 16); nk0 = new("f32", 1); t16 = new("f32", 16); t16b = new("f32", 16)
-    ts(iI, pI, 15, A.bitwise_and); ts(gI, pI, 4, A.arith_shift_right)
-    cp(cP, pI); cp(cI, iI); cp(cG, gI)
-    ts(cZ, gI, 16.0, A.mult, 15.0, A.add)
-    B, nB, G8, I, nI, nIbig, I64, nI4k, I2k, B2080, I3232, nTri, Wr, Ba, Bb, Ua, Lb, nIh = [new("bf", 128) for _ in range(18)]
-    B32 = new("f32", 128); Z = new("bf", 143); Zw = new("bf", 143)
-    Sel = new("bf", 2048); S = new("bf", 2048); ones = new("bf", 512)
-    io128 = sub(iof, 0, 128); io16 = sub(iof, 0, 16); k0 = sub(eqk, 0, 1); one128 = sub(ones, 0, 128)
     MAGIC = 12582912.0
-    ts(B, xh, cG, A.is_equal)
+    cP, cH, c16, cI, cW, cS = [new("f32", 1) for _ in range(6)]
+    xh = new("bf", 128); iob = new("bf", M); posT = new("bf", M); io16 = new("bf", 16)
+    iota(cP, [[0, 1]], 0, 1)
+    iota(xh, [[16, 8], [0, 16]], 0, 0)
+    iota(io16, [[1, 16]], 0, 0)
+    iota(sub(iob, 0, 144), [[1, 144]], 0, 0)
+    iota(sub(iob, 144, M), [[1, M - 144]], 144, 0)
+    iota(posT, [[1, 128], [128, 2]], 0, 0)
+    eqk = new("f32", 16); t16 = new("f32", 16); t16b = new("f32", 16)
+    ts(cH, cP, -7.5, A.add, 0.0625, A.mult)
+    ts(c16, cH, MAGIC, A.add, MAGIC, A.subtract)
+    lin(cH, c16, scale=16.0); c16 = cH
+    tt(cI, cP, c16, A.subtract)
+    (B, nB, G8, I, nI, nIbig, nI32, nI4032, nI127, nTri, Wr, M1, Bw, Bs, BD, I3232, I2080, I16k, I14k, nB2k, B8k, nIh, eps,
+     zero) = [new("bf", 128) for _ in range(24)]
+    B32 = new("f32", 128); Z = new("bf", 143); Zw = new("bf", 143); Sel = new("bf", 2048)
+    io128 = sub(iob, 0, 128)
+    add("v", lambda q: q.memset(ap(zero), 0.0), [], [zero], OV + 64 * CY, early=1)
+    ts(B, xh, c16, A.is_equal)
     ts(eqk, io16, cI, A.is_equal)
-    ts(Z, sub(iof, 0, 143), cZ, A.is_equal)
+    ts(Z, sub(iob, 0, 143), c16, A.subtract, 15.0, A.is_equal)
     ts(I, io128, cP, A.is_equal)
     for k in range(16):
-        lin(sub(Sel, 128 * k, 128 * k + 128), B, scale=sub(eqk, k, k + 1))
+        o = sub(Sel, 128 * k, 128 * k + 128)
+        either(lambda: lin(o, B, scale=sub(eqk, k, k + 1)), lambda: asel(o, B, [[16, 8], [0, 16]], A.is_equal, k, -1))
+    Sel0 = sub(Sel, 0, 128)
     ts(t16, io16, cI, A.is_lt, 1.0, A.add)
     add("v", lambda q: q.tensor_reduce(ap(cW), ap(t16), AxisListType.X, A.mult), [t16], [cW], 110.0)
     ts(t16b, io16, cI, A.is_gt, 1.0, A.add)
     add("v", lambda q: q.tensor_reduce(ap(cS), ap(t16b), AxisListType.X, A.mult), [t16b], [cS], 110.0)
-    lin(Zw, Z, scale=cW)
-    if any(CFG["bits"]):
-        lin(cD, cS, scale=2.0 ** -16); lin(cU, cW, scale=2.0); lin(cM, cW, scale=-2.0 * MAGIC)
-    for o, x, s in ((nB, B, -1.0), (nI, I, -1.0), (I64, I, 2.0 ** -6), (nIbig, I, -65536.0), (nI4k, I, -4096.0), (I2k, I, 2048.0),
-                    (B2080, B, 2080.0), (I3232, I, 3232.0), (B32, B, 1.0), (Ba, B, 1.5), (Bb, B, 0.05), (nk0, k0, -1.0), (nIh, I, -0.5)):
-        lin(o, x, scale=s)
-    ts(G8, xh, cP, A.is_equal)
-    zero = new("bf", 256)
-    add("v", lambda q: q.memset(ap(zero), 0.0), [], [zero], OV + 128 * CY, early=1)
-    act(sub(ones, 0, 256), zero, F.Exp, extra=1600.0); ops[-1]["early"] = 1
-    copy(sub(ones, 256, 512), sub(ones, 0, 256))
+    for o, x, s in ((Zw, Z, cW), (nB, B, -1.0), (nI, I, -1.0), (B32, B, 1.0), (nIbig, I, -65536.0),
+                    (I2080, I, 2080.0 * 128), (I3232, I, 3232.0), (Bs, B, cS), (I14k, I, 14336.0), (nI32, I, -32.0), (nI4032, I, -4032.0),
+                    (Bw, B, cW), (I16k, I, 16384.0), (nB2k, B, -2048.0), (B8k, B, 8192.0), (nIh, I, -0.5), (nI127, I, -127.5)):
+        if x is I:
+            either(lambda: lin(o, x, scale=s), lambda: asel(o, zero, [[1, 128]], A.not_equal, 0, -1, s))
+        else:
+            lin(o, x, scale=s)
+    ts(G8, xh, 0.0625, A.mult, cP, A.is_equal)
+    act(eps, zero, F.Exp, bias=-4.852030264, extra=1600.0); ops[-1]["early"] = 1
     asel(nTri, nB, [[1, 128]], A.is_gt, 0, -1)
-    for b in range(4):
-        asel(sub(S, 512 * b, 512 * b + 512), ones, [[1, 32], [0, 16]], A.is_equal, 32 * b, -1)
-    asel(Ua, Ba, [[1, 128]], A.is_gt, 0, -1); asel(Lb, Bb, [[-1, 128]], A.is_gt, 0, 1)
-    tt(Wr, Ua, Lb, A.add)
-    Gw = [new("bf", M), new("bf", M)]
-    for w in Gw:
-        iota(w, [[1, M]], 0, 0)
-    nI32 = new("f32", 128)
-    if 2 in CFG["bits"]:
-        lin(nI32, I, scale=-1.0)
+    lin(Wr, mm1([(I, B), (nI32, nTri)]), scale=0.05)
+    lin(M1, mm1([(I, I16k), (I, B8k)]))
+    lin(BD, mm1([(Bs, I)]), scale=2.0 ** -16)
+    Gw = [new("bf", M) for _ in range(3)]
+    for a in (0, 1):
+        copy(half(Gw[a], 1 - a), half(iob, 1 - a))
+    lin(half(Gw[2], 1), half(iob, 1), scale=2.0, bias=-255.0)
 
     def W(j, z=Z):
         return sub(z, 15 - j, 143 - j)
 
-    thb = sub(zero, 0, 8)
+    thb = new("bf", 16)
+    add("v", lambda q: q.memset(ap(thb), 0.0), [], [thb], OV + 64 * CY)
     add("v", lambda q: q.tensor_copy(T.bf[0:8, thb[1]:thb[1] + 2], T.thi[0:8, 0:2]), [thi, thb], [thb], 110.0)
+    p = mm1([(G8, thb)], 16)
+    lin(sub(XB[0], TO, TO + 1), sub(p, 0, 1), scale=-1.0, bias=64.0)
+    lin(sub(XB[0], TO + 1, XO), sub(p, 1, 16), bias=-127.0)
 
     ptu = new("u16", 16); Pn = new("bf", M)
-    cp(ptu, pti); ts(Cf, cqi, -2048.0, A.add)
-    lin(Pn, [iof, ptu])
+    cp(ptu, pti)
+    ts(half(Ct, 1), sub(cqi, 1, M, 2), S0, A.add)
+    lin(Pn, [posT, ptu])
     L = [new("u16", 16) for _ in range(3)]; PS = [new("bf", M) for _ in range(4)]
+    p = slot(16)
+    mm([(sub(p, 8 * a, 8 * a + 8), [(W(i), sub(Pn, 2 * i + a, M, 32)) for i in range(16)]) for a in (0, 1)])
+    ts(L[0], p, 0.0625, A.mult)
     for a in (0, 1):
-        p = mm1([(W(i), sub(Pn, 2 * i + a, M, 32)) for i in range(16)], 8)
-        ts(sub(L[0], 8 * a, 8 * a + 8), p, 0.0625, A.mult)
-        lin(sub(PS[0], 128 * a, 128 * a + 128), sub(Pn, a, M, 2))
-    lin(sub(XB[0], V + H, XW), mm1([(G8, thb)], 8))
+        copy(half(PS[0], a), sub(Pn, a, M, 2))
 
-    nb = [0]; nr = [0]
+    Dn = new("f16", M); En = new("bf", M); upn = new("f32", M)
+    ts(Dn, cqi, -2048.0, A.add)
+    ts(En, Dn, 2047.0, A.is_equal, 2.0 ** -6, A.mult)
+    ts(upn, [cqi, ptu], NO - 0.5, A.min, -2048.0, A.add)
 
-    def bits(out, x):
-        k = nb[0]; nb[0] += 1
-        if CFG["bits"][k]:
-            n1 = new("f32", 128); n2 = new("f32", 128)
-            p = mm1([(B, x), (I64, one128)])
-            act(n1, p, F.Identity, bias=MAGIC, scale=cD, v=(cD, A.mult, MAGIC, A.add))
-            act(n2, n1, F.Identity, bias=cM, scale=cU, v=(cU, A.mult, cM, A.add))
-            if CFG["bits"][k] == 1:
-                tt(out, p, n2, A.is_lt)
+    def bits(out, x, p):
+        rn = new("f32", 128)
+        mm([(p, [(BD, x), (BD, eps)])])
+        ts(rn, p, MAGIC, A.add, MAGIC, A.subtract)
+        tt(out, p, rn, A.is_lt)
+
+    def relation(n, Lst, old=None):
+        a = n & 1
+        R = {k: new("bf", 128) for k in ("E", "Pm", "inC")}
+        eqb = new("bf", 2048); La = sub(Lst, 8 * a, 8 * a + 8); w = CFG["eqw"][n]
+        upr = new("f32", w)
+        if old is None:
+            R["Dm"] = sub(Dn, a, M, 2); R["E"] = sub(En, a, M, 2)
+            if w > 128:
+                copy(sub(upr, 0, 128), sub(upn, a, M, 2))
             else:
-                act(out, mm1([(B, x), (I64, one128), (nI32, n2)]), F.Relu, scale=-1.0)
-                act(out, out, F.Sign, v=(0.0, A.is_gt))
+                upr = sub(upn, a, M, 2)
         else:
-            bI = new("i32", 128); bJ = new("i32", 128)
-            ts(bI, mm1([(B, x)]), cS, A.mult); ts(bJ, bI, 32768, A.bitwise_and); ts(out, bJ, 2.0 ** -15, A.mult)
-
-    def relation(a, Lst):
-        R = {k: new("bf", 128) for k in ("E", "Pm", "out", "fe", "inC", "inT")}
-        R["Dm"] = new("f16", 128); R["FC"] = new("f16", 128); R["xl"] = new("f16", 8)
-        eqb = new("bf", 2048); Ca = sub(Cf, a, M, 2); La = sub(Lst, 8 * a, 8 * a + 8)
-        relu(R["E"], Ca, -2046.0)
-        cp(R["Dm"], Ca)
-        diff = CFG["diff"][nr[0]]; nr[0] += 1
-        if diff:
-            uph = new("f16", 128); upe = new("bf", 128)
-            cp(uph, [Cf, La])
-            ts(upe, uph, 2047.0, A.is_equal)
-        else:
-            upr = new("f32", 512); u0 = new("f32", 128)
-            act(u0, [Cf, La], F.Relu, bias=2046.5, scale=-1.0, v=(2046.5, A.min, -1.0, A.mult))
-            u0v = ops[-1]
-            del u0v["alt"]["v"]
-            lin(sub(upr, 0, 128), u0, scale=-1.0, bias=2046.5)
-            for u in (1, 2, 3):
-                if CFG["up3"]:
-                    copy(sub(upr, 128 * u, 128 * u + 128), sub(upr, 0, 128))
-            if not CFG["up3"]:
-                copy(sub(upr, 128, 256), sub(upr, 0, 128))
-                copy(sub(upr, 256, 512), sub(upr, 0, 256))
-        Pk = slot(128, True)
+            R["Dm"] = new("f16", 128)
+            ts(R["Dm"], half(Ct, a), S0 + NO, A.min, -S0 - 2048, A.add)
+            ts(R["E"], R["Dm"], 2047.0, A.is_equal, 2.0 ** -6, A.mult)
+            ts(sub(upr, 0, 128), [Ct, La], S0 + NO - 0.5, A.min, -S0 - 2048, A.add)
+        u = 128
+        while u < w:
+            copy(sub(upr, u, 2 * u), sub(upr, 0, u)); u *= 2
+        Pk = slot(128, True); Ic = slot()
         for c in range(4):
             bc = slot(512); eq = sub(eqb, 512 * c, 512 * c + 512)
-            more = [(nI, uph), (nI4k, upe)] if diff else []
-            mm([(sub(bc, 128 * u, 128 * u + 128), [(sub(Sel, 128 * (4 * c + u), 128 * (4 * c + u + 1)), R["Dm"])] + more) for u in range(4)])
-            if diff:
-                ts(eq, bc, 0.0, A.is_equal)
-            else:
-                tt(eq, bc, upr, A.is_equal)
-            terms = [(W(4 * c + u, Zw), sub(eq, 128 * u, 128 * u + 128)) for u in range(4)]
-            mm([(Pk, ([(I64, R["E"])] if c == 0 else []) + terms)], first=c == 0, last=c == 3)
-        act(R["out"], Pk, F.Relu, bias=1.0, scale=-64.0, v=(0.0, A.is_equal))
-        lin(R["Pm"], Pk)
-        first = mm1([(I, R["out"]), (nTri, R["out"])])
-        relu(first, first)
-        R["NH0"] = mm1([(B, R["out"])])
-        act(R["NH0"], R["NH0"], F.Relu, bias=k0, scale=nk0, v=(0.0, A.is_equal, k0, A.mult))
-        tt(R["FC"], first, R["Dm"], A.mult)
-        cp(R["xl"], mm1([(W(i), sub(R["FC"], i, 128, 16)) for i in range(16)], 8))
-        bits(R["inC"], R["Pm"])
-        relu(R["fe"], mm1([(I, R["E"]), (nTri, R["E"])]))
-        lin(R["inT"], mm1([(R["inC"], I)]))
+            mm([(half(bc, u), [(half(Sel, 4 * c + u), R["Dm"])]) for u in range(4)])
+            for u in range(0, 512, w):
+                tt(sub(eq, u, u + w), sub(bc, u, u + w), upr, A.is_equal); row("eq", 2048 * n + 512 * c + u)
+            terms = [(W(4 * c + u, Zw), half(eq, u)) for u in range(4)]
+            mm([(Pk, ([(I, R["E"])] if c == 0 and old is None else []) + terms)], first=c == 0, last=c == 3)
+        if old is None:
+            R["out"] = new("bf", 128); R["xB"] = new("f16", 128); R["yl"] = new("u16", 16); R["inT"] = new("bf", 128)
+            FC = new("f32", 128); r16 = new("bf", 128)
+            either(lambda: act(R["out"], Pk, F.Relu, bias=4096.0, scale=-262144.0), lambda: ts(R["out"], Pk, 0.0, A.is_equal, 4096.0, A.mult))
+            relu(FC, mm1([(nI, R["Dm"]), (nTri, R["out"]), (I, R["out"])]), -2048.0)
+            relu(r16, mm1([(I, io128), (nB, R["out"])]), scale=16.0)
+            ts(R["xB"], mm1([(nI, r16), (B32, FC)]), -1.0, A.mult, 2048.0, A.add)
+            ts(R["yl"], mm1([(W(i), sub(R["xB"], i // 2, 128, 8)) for i in range(16)], 16), 0.0625, A.mult, 2048.0, A.add)
+        else:
+            for k in ("out", "xB", "yl", "inT"):
+                R[k] = old[k]
+        lin(R["Pm"], Pk, bias=2.0 ** -9)
+        if CFG["inc"][n]:
+            mm([(Ic, [(I, half(eqb, k)) for k in range(16)])])
+            lin(R["inC"], Ic)
+        else:
+            bits(R["inC"], R["Pm"], Ic)
+        if old is None:
+            lin(R["inT"], mm1([(R["inC"], I)]))
         return R
 
     def acting(R, t):
         a = t & 1
-        for k in ("act", "gone", "mJ0"):
+        for k in ("nact", "gone", "fe"):
             R[k] = new("bf", 128)
-        R["Cn0"] = new("f32", 128); r0 = new("f32", 128)
-        lin(R["act"], [par, sub(L[t], 8 * a, 8 * a + 8)], scale=1.0 - 2 * a, bias=float(a))
-        relu(R["gone"], mm1([(I, R["act"]), (nB, R["out"])]))
-        p = mm1([(I, sub(PS[t], 128 * a, 128 * a + 128)), (nI, sub(ioP, 128 * a, 128 * a + 128))])
-        gd = new("bf", 128)
-        tt(gd, p, R["gone"], A.mult)
-        lin(sub(Gw[a], a, M, 2), mm1([(I, gd), (I, sub(ioP, 128 * a, 128 * a + 128))]))
-        lin(PS[t + 1], [Gw[a], L[t]])
+        R["capA"] = new("f32", 128); gd = new("bf", 128)
+        ts(R["nact"], half(PS[t], a), 127.5, A.is_gt if a else A.is_lt, -32.0, A.mult)
+        relu(R["gone"], mm1([(I, R["nact"]), (nB, R["out"])]), 1.0)
+        tt(gd, mm1([(I, half(PS[t], a)), (nI, half(iob, a))]), R["gone"], A.mult)
+        if t < 2:
+            lin(half(Gw[t], a), mm1([(I, gd), (I, half(iob, a))]))
+        else:
+            lin(half(Gw[t], a), mm1([(I, gd), (I, half(iob, a)), (nI127, R["gone"])]), scale=2.0)
+        lin(PS[t + 1], [Gw[t], L[t]])
         if t < 2:
             ts(L[t + 1], mm1([(W(i), sub(PS[t + 1], i, M, 16)) for i in range(16)], 16), 0.0625, A.mult)
         else:
             lin(ypo, mm1([(W(i), sub(PS[3], (i & 1) * 128 + (i >> 1), (i & 1) * 128 + 128, 8)) for i in range(16)], 16), scale=0.0625)
             dma("s", T.yp[:], T.ypo[:], [ypo], [], "op", 2000.0)
-        relu(r0, mm1([(nI, R["Dm"]), (nI4k, R["gone"])]), 2047.0)
-        lin(R["Cn0"], r0, scale=-1.0, bias=4095.0 if t == 2 else 2047.0)
 
-    def onehots(t, lo, hi):
-        paT = new("f32", 16); w = hi - lo; OH = new("bf", 16 * w)
+    def rooms(R):
+        relu(R["fe"], mm1([(I, R["E"]), (nTri, R["E"]), (nI, R["gone"])]), scale=64.0)
+        lin(R["capA"], mm1([(I, R["Dm"]), (nIbig, R["fe"]), (nIbig, R["gone"])]), bias=S0 + 2048)
+
+    def onehots():
+        paT = new("f32", 16); OH = new("bf", 16 * M)
         p = slot(16)
-        mm([(sub(p, 8 * ch, 8 * ch + 8), [(sub(PS[t], 128 * ch, 128 * ch + 128), sub(I, 0, 128, 16))]) for ch in (0, 1)])
+        mm([(sub(p, 8 * ch, 8 * ch + 8), [(half(PS[0], ch), sub(I, 0, 128, 16))]) for ch in (0, 1)])
         lin(paT, p)
         for u in range(16):
-            ts(sub(OH, w * u, w * u + w), sub(ioP, lo, hi), sub(paT, u, u + 1), A.is_equal)
-        return lambda ch, gr, a: sub(OH, w * (8 * ch + gr) + 128 * a - lo, w * (8 * ch + gr) + 128 * a - lo + 128)
+            if CFG["oh"]:
+                for a in (0, 1):
+                    ts(half(OH, 2 * u + a), half(iob, a), sub(paT, u, u + 1), A.is_equal); row("oh%d" % a, u)
+            else:
+                ts(sub(OH, M * u, M * u + M), iob, sub(paT, u, u + 1), A.is_equal); row("oh", u)
+        return lambda ch, gr, a: half(OH, 2 * (8 * ch + gr) + a)
 
     def leaving(R, t, oh, marks):
         a = t & 1
-        kb = new("bf", 128); Pc = new("bf", 128); can = new("bf", 128); R["can"] = can
+        kb = new("bf", 128); Pc = new("bf", 128); rn = new("f32", 128); R["can"] = new("bf", 128); R["sg"] = new("bf", 128)
         p = slot()
         mm([(sub(p, 16 * gr, 16 * gr + 16), [(oh(ch, gr, a), sub(marks[ch], 16 * gr, 16 * gr + 16)) for ch in (0, 1)]) for gr in range(8)])
         lin(kb, p)
         relu(Pc, mm1([(kb, nIbig), (I, R["Pm"])]))
-        bits(can, Pc)
-        R["sg"] = mm1([(I, can), (I, R["act"]), (nI, R["gone"])])
-        act(R["sg"], R["sg"], F.Sign, bias=1.5, scale=-1.0)
+        bits(R["can"], Pc, slot())
+        act(R["sg"], mm1([(I, R["can"]), (nI, R["gone"])]), F.Sign, bias=0.5, scale=-1.0)
 
-    Qu = new("u16", 128); hu = new("u16", 128); ylu = new("u16", 8); Qh = new("f16", 128); rq = new("f16", 128)
-    pp = new("f32", 128); Qn = new("f32", 128); nI_ = new("i32", 128); hI = new("i32", 128)
-    Xy = new("bf", 128); XyT = new("bf", 128); XQ = new("bf", 2048); Cmp = new("bf", 2048); ad = new("f32", 2048)
+    Qu = new("u16", 128); hu = new("u16", 128); Qh = new("f16", 128); wq = new("f16", 128)
+    yv, pp, cap, fin = [new("f32", 128) for _ in range(4)]; uu0 = new("bf", 128); pen = new("bf", 128)
+    nI_ = new("i32", 128); hI = new("i32", 128)
+    Xy = new("bf", 256); Cmp = new("bf", 2048); ad = new("f32", 2048)
+    preJ, tw, ws, keep, eqL = [new("bf", 128) for _ in range(5)]
     odd = [None, new("i32", 1), new("i32", 1)]
 
-    def front(R, t):
-        a = t & 1; La = sub(L[t], 8 * a, 8 * a + 8); xw = sub(XB[t], 0, V); lw = sub(XB[t], V, V + H)
-        cp(Qh, [Cf, La])
-        ts(Qu, Qh, 2048.0, A.add)
-        tt(rq, R["NH0"], Qh, A.mult)
-        yl = mm1([(I, R["xl"])] + [(W(i), sub(rq, i, 128, 16)) for i in range(16)], 8)
-        y = mm1([(B, R["FC"]), (B, rq)])
-        lp = mm1([(B2080, R["FC"]), (B2080, rq), (I3232, Qh)])
-        tt(pp, y, Qh, A.mult)
-        tt(nI_, lp, pp, A.add)
+    def front(R, t, Lst):
+        a = t & 1; La = sub(Lst, 8 * a, 8 * a + 8); xw = sub(XB[t], XO, QO); lw = sub(XB[t], 0, H); XQ = sub(XB[t], QO, XW)
+        if t == 0:
+            ts(Qu, sub(upn, 0, M, 2), 2048.25, A.add)
+        else:
+            ts(Qu, [Ct, La], S0 + NO, A.min, -S0, A.add)
+        ts(Qh, Qu, -2048.0, A.add)
+        tt(yv, mm1([(Sel0, Qh), (B, R["out"])]), R["xB"], A.min)
+        q32 = mm1([(I, Qh), (I2080, eps)])
+        tt(pp, q32, yv, A.mult)
+        tt(nI_, mm1([(I3232, Qh)]), pp, A.add)
         ts(hI, nI_, 5, A.arith_shift_right, H - 1, A.bitwise_and)
         cp(hu, hI)
-        ts(ylu, yl, 2048.0, A.add)
-        lin(Xy, [xw, ylu])
-        lin(XyT, mm1([(Xy, nI)]))
+        tt(cap, mm1([(I, Qh), (I14k, R["gone"])]), R["capA"], A.max)
         c0 = 0
-        for w in CFG["chunks"]:
-            c1 = c0 + w
-            lin(sub(XQ, c0, c1), [xw, sub(Qu, c0 // 16, c1 // 16)])
-            d = mm1([(I, sub(XQ, c0, c1)), (XyT, sub(S, c0, c1))], w)
-            act(sub(ad, c0, c1), d, F.Abs)
-            tt(sub(Cmp, c0, c1), [lw, sub(hu, c0 // 16, c1 // 16)], sub(ad, c0, c1), A.is_ge)
-            c0 = c1
-        lin(Qn, [Cf, La], scale=-1.0, bias=2047.0)
+        for m, w in enumerate(CFG["chunks"][t]):
+            c1 = c0 + w; xy = sub(Xy, c0 // 8, c1 // 8); xq = sub(XQ, c0, c1); d = slot(w, True)
+            lin(xq, [xw, sub(Qu, c0 // 16, c1 // 16)])
+            if m not in CFG["xqv"][t]:
+                row("s%d" % t, 2 * m - 2.5, "a")
+            else:
+                row("v%d" % t, -1, "v")
+            lin(xy, [sub(XB[t], XO, QO + c1), sub(R["yl"], c0 // 128, c1 // 128)])
 
-    nfs, preJ, pre0, gg, tw, ws, mk, rw, nk, zb = [new("bf", 128) for _ in range(10)]
-    uu, QS, wq, Cn2, vc = [new("f32", 128) for _ in range(5)]
+            def fn(q, d=d, xq=xq, xy=xy, w=w):
+                q.matmul(ap(d), ap(I), ap(xq), True, False)
+                for u in range(8):
+                    ins = q.matmul(ap(sub(d, u, w, 8)), ap(nI), ap(xy), False, u == 7)
+                return ins
+            add("p", fn, [I, nI, xq, xy], [d], 30 + PE * (w + 8 * max(64, w // 8)))
+            act(sub(ad, c0, c1), d, F.Abs); row("s%d" % t, 2 * m)
+            tt(sub(Cmp, c0, c1), [lw, sub(hu, c0 // 16, c1 // 16)], sub(ad, c0, c1), A.is_ge); row("v%d" % t, m)
+            c0 = c1
 
     def decide(R, t):
         a = t & 1
-        c1 = new("f32", 1); c2 = new("f32", 1); th1 = sub(XB[t], V + H, V + H + 1); th2 = sub(XB[t], V + H + 1, V + H + 2)
-        lin(c2, th2, scale=-1.0, bias=-20.0)
+        c1 = new("f32", 1); th1 = sub(XB[t], TO, TO + 1); th2 = sub(XB[t], TO + 1, TO + 2)
         if t == 0:
-            lin(c1, th1, scale=-1.0, bias=40.0)
+            lin(c1, th1)
         else:
-            c0 = new("f32", 1)
-            tt(c0, odd[t], th1, A.add)
-            lin(c1, c0, scale=-1.0, bias=40.0)
-        lin(pre0, R["gone"], scale=c2, bias=-40.0)
-        nc1 = new("f32", 1)
-        lin(nc1, c1, scale=-1.0)
-        act(nfs, Qn, F.Relu, bias=1.0, scale=-1.0, v=(0.0, A.is_equal))
-        act(preJ, mm1([(I, R["act"]), (nI, R["gone"]), (B, R["fe"]), (nI, R["inC"]), (nI, nfs)]), F.Relu, bias=nc1, scale=c1,
-            v=(1.5, A.is_gt, c1, A.mult))
-        tt(QS, R["sg"], Qn, A.mult)
-        z = slot(); vm = slot()
-        mlast = 128 - CFG["chunks"][-1] // 16
-        for m0, m1 in ((0, mlast), (mlast, 128)):
-            mm([(sub(z, m0, m1), [(I, sub(pre0, m0, m1)), (I, sub(preJ, m0, m1))] +
-                 [(W(j), sub(Cmp, 16 * m0 + j, 16 * m1, 16)) for j in range(16)])])
-        ts(gg, z, 0.0, A.is_ge, 41.0, A.mult)
-        tt(zb, z, gg, A.add)
-        tt(uu, R["sg"], zb, A.mult)
-        act(tw, uu, F.Exp, bias=-117.5, scale=3.4657359)
-        act(nk, zb, F.Sign, bias=59.5)
-        tt(Cn2, mm1([(I, Qh), (I2k, nk)] + [(I2k, one128)] * (2 if t == 2 else 1)), R["Cn0"], A.min)
-        Kp = mm1([(nI, R["Dm"]), (nI, R["fe"]), (I2k, one128)] if CFG["vc"][t] else [(I, R["Dm"]), (I, R["fe"])])
-        X = mm1([(Wr, tw)])
-        tt(X, X, tw, A.is_lt)
-        tt(wq, X, QS, A.mult)
-        v = mm1([(B32, wq)])
-        if CFG["vc"][t]:
-            act(vc, v, F.Relu, bias=1.0, scale=-1.0)
-        else:
-            ts(vc, v, 1.0, A.min, 2047.0, A.add)
-        tt(mk, Kp, vc, A.is_equal)
-        tt(vm, v, mk, A.mult)
-        tt(sub(Yc if t == 2 else Cf, a, M, 2), Cn2, vm, A.subtract)
+            ts(c1, odd[t], -1.0, A.mult, th1, A.add)
+        ts(preJ, mm1([(B8k, R["fe"]), (nIbig, R["inC"]), (nI, Qh)]), 6145.5, A.is_gt, c1, A.mult)
+        z = slot(128, True)
+        mm([(z, [(nI4032, eps), (I, R["nact"]), (nI32, R["gone"]), (nI32, R["gone"])])], last=False)
+        cuts = CFG["zcut"][t]
+        for m0, m1 in zip(cuts, cuts[1:]):
+            if m1 == 128:
+                mm([(z, [(nI32, R["sg"]), (I, preJ)])], first=False, last=False)
+            mm([(sub(z, m0, m1), [(W(j), sub(Cmp, 16 * m0 + j, 16 * m1, 16)) for j in range(16)])], first=False, last=m1 == 128)
+        tt(uu0, z, R["sg"], A.mult)
+        either(lambda: act(pen, z, F.Relu, scale=-128.0), lambda: ts(pen, z, 0.0, A.min, -128.0, A.mult))
+        act(tw, mm1([(I, uu0), (nI, pen)]), F.Exp, bias=22.8, scale=3.4657359)
+        either(lambda: act(keep, z, F.Relu, bias=th2, scale=-1.0), lambda: ts(keep, z, th2, A.is_lt))
+        tt(ws, mm1([(Wr, tw)]), tw, A.is_lt)
+        tt(wq, mm1([(I, Qh)]), ws, A.mult)
+        tt(eqL, mm1([(Bw, ws)]), R["Pm"], A.is_equal)
+        v = slot(128, True)
+        mm([(v, [(I16k, R["fe"]), (I16k, R["gone"]), (nIbig, keep), (nB2k, ws)])], last=False)
+        mm([(v, [(B, wq)])], first=False, last=False)
+        mm([(v, [(M1, eqL)])], first=False)
         if t == 2:
+            tt(fin, v, cap, A.max)
+            ts(sub(Yc, a, M, 2), fin, S0 + NO, A.min, -S0, A.add)
             return None
-        act(ws, wq, F.Sign)
-        cT = new("bf", 128); jc = new("f32", 1); jb = new("bf", 1); oI = new("i32", 1)
-        relu(cT, mm1([(R["inC"], I), (R["can"], nIh), (R["gone"], nIh), (nk, nIh), (ws, I)]), 0.5)
-        act(rw, ws, F.Relu, acc=jc); lin(jb, jc)
-        cp(oI, mm1([(one128, jb)], 1)); ts(odd[t + 1], oI, 1, A.bitwise_and)
+        tt(half(Ct, a), v, cap, A.max)
+        cT = new("bf", 128); jb = new("bf", 1); oI = new("i32", 1); e1 = sub(eps, 0, 1)
+        act(cT, mm1([(R["inC"], I), (ws, nI), (R["can"], nI), (R["sg"], nIh), (keep, I)]), F.Abs, bias=0.5)
+        lin(jb, mm1([(ws, e1), (eqL, e1)], 1), scale=16384.0)
+        cp(oI, mm1([(eps, jb)], 1)); ts(odd[t + 1], oI, 1, A.bitwise_and)
         return cT
 
+    RT = routes(T, topo); got = arrivals(RT, T.cores[rank]); net = PAR["net"]
+
+    def send(k, sbuf, pc, wait, dst, dbuf, sem, mask):
+        rid, pid, _ = topo.addr(dst); a, b = pc
+        add("g", lambda q: q.remote_dma(T[dbuf][:, a:b], T[sbuf][:, a:b], T.sem[sem], T.sem.sent, pid, rid, mask),
+            [(sbuf, a, b, 1)], [("net", k, k + 1, 1)], PAR["rc"], remote=nbits(mask))
+        row("net", k)
+
+    def arrive(sem, s, a, b, k, lat):
+        add("x", None, [("net", 0, k, 1)], [sub(XB[s], a, b)], 0.0, sem=sem, inc=got[sem], lat=lat)
+    for k, w in enumerate(RT[T.cores[rank]]):
+        if k == 8:
+            arrive("af", 2, lmp[3][0], XO, 8, net[0])
+        send(k, *w)
+    arrive("ax1", 1, XO, QO, 4, net[1]); arrive("al1", 1, 0, XO, 9, net[2])
+    arrive("ax2", 2, XO, QO, 10, net[3]); arrive("al2", 2, 0, lmp[3][0], 10, net[3])
+
     R0 = relation(0, L[0])
+    acting(R0, 0); rooms(R0)
     R1 = relation(1, L[0])
-    acting(R0, 0)
-    oh0 = onehots(0, 0, 128 if CFG["oh"] else 256)
-    leaving(R0, 0, oh0, [R0["inT"], R1["inT"]])
-    acting(R1, 1)
-    front(R0, 0)
+    oh = onehots()
+    leaving(R0, 0, oh, [R0["inT"], R1["inT"]])
+    acting(R1, 1); rooms(R1)
+    front(R0, 0, L[0])
     cT0 = decide(R0, 0)
-    if CFG["oh"]:
-        oh0 = onehots(0, 128, 256)
-    leaving(R1, 1, oh0, [cT0, R1["inT"]])
-    R2 = relation(0, L[1])
-    acting(R2, 2)
-    oh1 = onehots(1, 0, 128)
-    front(R1, 1)
+    leaving(R1, 1, oh, [cT0, R1["inT"]])
+    R2 = relation(2, L[1], R0)
+    acting(R2, 2); rooms(R2)
+    front(R1, 1, L[0])
     cT1 = decide(R1, 1)
-    lin(sub(Yc, 1, M, 2), sub(Cf, 1, M, 2), bias=2048.0)
-    leaving(R2, 2, oh1, [R2["inT"], cT1])
-    front(R2, 2)
+    ts(sub(Yc, 1, M, 2), half(Ct, 1), S0 + NO, A.min, -S0, A.add)
+    leaving(R2, 2, oh, [R0["inT"], cT1])
+    front(R2, 2, L[1])
     decide(R2, 2)
     dma("s", T.yc[:], T.Yc[:], [Yc], [], "oc", 2500.0)
-
-    hs = helpers_of(T, topo, rank); d1 = T.cores[(rank - 1) % n]
-
-    def send(dst, buf, a, b, sem, mask, due):
-        rid, pid, _ = topo.addr(dst)
-        add("g", lambda q: q.remote_dma(T[buf][:, a:b], T.XB0[:, a:b], T.sem[sem], T.sem.sent, pid, rid, mask),
-            [sub(XB[0], a, b), S, nTri], [], 500.0, remote=nbits(mask), lat=due)
-    for pc, hsem, asem in ((xsp, "hx", "ax1"), (lmp, "hl", "al1")):
-        for k, hc in enumerate(hs):
-            send(hc, "XB0", pc[k][0], pc[k][1], hsem, topo.mask(me, hc) & ~topo.mask(me, d1), 38000.0)
-        send(d1, "XB1", pc[3][0], pc[3][1], asem, topo.mask(me, d1), 38000.0)
-    d2 = T.cores[(rank - 2) % n]
-    for pc, asem in ((xsp, "ax2"), (lmp, "al2")):
-        send(d2, "XB2", pc[3][0], pc[3][1], asem, topo.mask(me, d2), 30000.0)
     for k in nxt:
         assert nxt[k] <= SCRATCH[k][1][1], (k, nxt[k])
     return ops, temps
@@ -672,6 +715,163 @@ def search(ops, temps, iters, seed):
     return best
 
 
+def anneal(ops, temps, order, eng, iters, seed):
+    deps, succ, tmp, users = graph(ops, temps); n = len(ops); same, cross = PAR["same"], PAR["cross"]
+    before = [set(d) for d in deps]; after = [set(s) for s in succ]
+    for kind in ([i for i in range(n) if "remote" in ops[i]], [i for i in range(n) if "s" in ops[i]["alt"] and not ops[i]["rd"]]):
+        for i, j in zip(kind, kind[1:]):
+            before[j].add(i); after[i].add(j)
+    pre = [[(j, ops[j]["lat"]) for j in d] for d in deps]; cost = [{q: a[1] for q, a in o["alt"].items()} for o in ops]
+    lat = [o["lat"] for o in ops]; nuse = {t: len(users[t]) for t in temps}; x = [seed]; wide = CFG["wide"]
+    rem = [i for i in range(n) if "remote" in ops[i]]
+
+    def rnd(k):
+        x[0] = (x[0] * 1103515245 + 12345) % 2147483648
+        return (x[0] >> 8) % k
+
+    def run(lst, eng, full=False):
+        end = [0.0] * n; crit = [-1] * n; free = dict.fromkeys("vapgsx", 0.0); last = dict.fromkeys("vapgsx", -1)
+        by = [-1] * 8; live = [0] * 8; tenant = [[None] * 4 for _ in range(8)]; todo = dict(nuse); gone = {}; place = {}
+        more = [set() for _ in range(n)] if full else None
+        for i in lst:
+            q = eng[i]; t = free[q]; c = last[q]; sq = 0.0 if q == "p" else same
+            for j, l in pre[i]:
+                u = end[j] + l + (cross if eng[j] != q else sq)
+                if u > t:
+                    t = u; c = j
+            for y in tmp[i]:
+                if y in place:
+                    b = place[y][0]; j = by[b]
+                    if eng[j] != q and end[j] + cross > t:
+                        t = end[j] + cross; c = j
+                else:
+                    best = None; whole = temps[y] == 4
+                    for b in range(8):
+                        k = live[b]
+                        if (k > 0) if whole else (k == 4 or b < wide):
+                            continue
+                        j = by[b]; u = t; s = 0
+                        if j >= 0 and eng[j] != q and end[j] + cross > u:
+                            u = end[j] + cross
+                        row = tenant[b]
+                        if whole:
+                            for w in row:
+                                if w is not None and gone[w] > u:
+                                    u = gone[w]
+                        else:
+                            m = None
+                            for s2 in range(4):
+                                w = row[s2]
+                                if w is None or todo[w] == 0:
+                                    g2 = 0.0 if w is None else gone[w]
+                                    if m is None or g2 < m:
+                                        m = g2; s = s2
+                            if m > u:
+                                u = m
+                        if best is None or u + 60 * k < best[0]:
+                            best = (u + 60 * k, u, b, s)
+                    if best is None:
+                        return None
+                    _, u, b, s = best
+                    if u > t:
+                        t = u; c = by[b]
+                    place[y] = (b, s); row = tenant[b]
+                    for s2 in range(s, s + temps[y]):
+                        if full and row[s2] is not None:
+                            more[i].update(users[row[s2]])
+                        row[s2] = y
+                    live[b] += temps[y]
+                if full and by[b] >= 0 and eng[by[b]] != q:
+                    more[i].add(by[b])
+            e = t + cost[i][q]; end[i] = e; crit[i] = c; free[q] = e; last[q] = i
+            for y in tmp[i]:
+                b = place[y][0]; by[b] = i; todo[y] -= 1; gone[y] = max(gone.get(y, 0.0), e + cross)
+                if todo[y] == 0:
+                    live[b] -= temps[y]
+        top = max(range(n), key=lambda i: end[i] + lat[i]); span = end[top] + lat[top]
+        if full:
+            return span, lst, [deps[i] | more[i] for i in range(n)], place, [end[i] - cost[i][eng[i]] for i in range(n)], eng
+        path = []
+        while top >= 0:
+            path.append(top); top = crit[top]
+        span += CFG["soon"] * sum(end[i] for i in rem)
+        return span + CFG["mean"] * sum(end) / n, path, span, end
+
+    lst = list(order); eng = list(eng); cur = run(lst, eng)
+    if cur is None:
+        return None
+    best = (cur[2], lst, eng)
+    for it in range(iters):
+        i = cur[1][rnd(len(cur[1]))] if rnd(10) < 6 else rnd(n)
+        l2 = lst; e2 = eng; kind = rnd(10)
+        if kind < 2 and len(cost[i]) > 1:
+            e2 = list(eng); qs = [q for q in cost[i] if q != eng[i]]; e2[i] = qs[rnd(len(qs))]
+        if kind >= 1:
+            p = lst.index(i); hops = 1 + rnd(5) * rnd(5) * rnd(2); step = -1 if rnd(10) < 6 else 1; r = p; q = e2[i]
+            while hops and 0 <= r + step < n:
+                r += step
+                if e2[lst[r]] == q:
+                    hops -= 1
+            rel = before if step < 0 else after
+            seg = lst[r:p] if step < 0 else lst[p + 1:r + 1]
+            pull = set(rel[i]); go = []; stay = []
+            for j in (reversed(seg) if step < 0 else seg):
+                if j in pull:
+                    go.append(j); pull |= rel[j]
+                else:
+                    stay.append(j)
+            if step < 0:
+                l2 = lst[:r] + go[::-1] + [i] + stay[::-1] + lst[p + 1:]
+            else:
+                l2 = lst[:p] + stay + [i] + go + lst[r + 1:]
+        new = run(l2, e2)
+        if new is not None and new[0] <= cur[0] + CFG["temp"] * (1 - it / iters) * rnd(100) / 100:
+            cur = new; lst = l2; eng = e2
+            if new[2] < best[0]:
+                best = (new[2], lst, eng)
+        if it % 16 == 0:
+            end = cur[3]; l2 = sorted(lst, key=lambda j: end[j] - cost[j][eng[j]]); new = run(l2, eng)
+            if new is not None and new[0] <= cur[0] + 20:
+                cur = new; lst = l2
+    return run(best[1], best[2], True)
+
+
+def make_plan(ops, temps):
+    deps, succ, _, _ = graph(ops, temps); n = len(ops); rows = {}
+    pred = [set(d) for d in deps]; nxt = [list(s) for s in succ]
+    for i, o in enumerate(ops):
+        for name, k in o.get("row", ()):
+            rows.setdefault(name, []).append((k, i))
+    for row in rows.values():
+        row.sort()
+        for (_, i), (_, j) in zip(row, row[1:]):
+            pred[j].add(i); nxt[i].append(j)
+    tail = {}
+
+    def far(i):
+        if i not in tail:
+            tail[i] = min(a[1] for a in ops[i]["alt"].values()) + ops[i]["lat"] + max([PAR["cross"] + far(k) for k in nxt[i]] + [0.0])
+        return tail[i]
+    for i in range(n - 1, -1, -1):
+        far(i)
+    key = [-1e9 if ops[i].get("early") else -tail[i] for i in range(n)]
+    best = search(ops, temps, CFG["iters"], CFG["seed"])
+    for pen in (200.0, 500.0, 1000.0, 2000.0):
+        st, en, eng = insert_schedule(ops, pred, nxt, key, [pen] * n, False)
+        late_psum(ops, nxt, st, en, eng)
+        left = [len(d) for d in pred]; ready = [i for i in range(n) if not left[i]]; order = []
+        while ready:
+            i = min(ready, key=lambda j: (st[j], j)); ready.remove(i); order.append(i)
+            for k in nxt[i]:
+                left[k] -= 1
+                if left[k] == 0:
+                    ready.append(k)
+        r = anneal(ops, temps, order, eng, 0, 1)
+        if r is not None and (best is None or r[0] < best[0]):
+            best = r
+    return anneal(ops, temps, best[1], best[5], CFG["moves"], CFG["seed"])
+
+
 def rank_program(g, core, T, topo):
     rank = T.rank_of(core)
     if rank is None:
@@ -680,8 +880,11 @@ def rank_program(g, core, T, topo):
     place = {}
     ops, temps = build(T, topo, rank, place)
     if not PLAN:
-        PLAN["x"] = search(ops, temps, CFG["iters"], CFG["seed"])
+        RT = routes(T, topo); r = max(range(len(T.cores)), key=lambda r: sum(w[2] is not None for w in RT[T.cores[r]]))
+        PLAN["x"] = make_plan(*build(T, topo, r, {}))
     _, order, deps, pl, _s, eng = PLAN["x"]
+    own = graph(ops, temps)[0]
+    deps = [own[i] if "remote" in ops[i] else deps[i] for i in range(len(ops))]
     place.update(pl)
     queue = {"v": g.vector, "a": g.scalar, "p": g.tensor, "g": g, "s": g.sync}
     semof = {"v": "sv", "a": "sa", "p": "sp", "g": "sg"}

from concourse.bass import DstId, RemoteDMATransfer
from concourse.mybir import dt, AluOpType, AxisListType, ActivationFunctionType

V, H, M, NO = 4096, 2048, 256, 4095
TO, XO = H, H + 16
QO = XO + V
XW = QO + 2048
NBF, NF32, NF16, NI32, NU16 = 36864, 10240, 2048, 2048, 1024
SCRATCH = {
    "XB0": ("sbuf", [128, XW], "bfloat16"), "XB1": ("sbuf", [128, XW], "bfloat16"), "XB2": ("sbuf", [128, XW], "bfloat16"),
    "cqi": ("sbuf", [128, M], "int32"), "pti": ("sbuf", [128, 16], "int32"), "thi": ("sbuf", [128, 8], "int32"),
    "Ct": ("sbuf", [128, M], "float32"), "Yc": ("sbuf", [128, M], "float32"), "ypo": ("sbuf", [128, 16], "float32"),
    "bf": ("sbuf", [128, NBF], "bfloat16"), "f32": ("sbuf", [128, NF32], "float32"), "f16": ("sbuf", [128, NF16], "float16"),
    "i32": ("sbuf", [128, NI32], "int32"), "u16": ("sbuf", [128, NU16], "uint16"),
}
for _b in range(8):
    SCRATCH["ps%d" % _b] = ("psum", [128, 512], "float32")
SEMAPHORES = ["sv", "sa", "sp", "sg", "lcq", "lpt", "lth", "oc", "op", "sent", "hx", "hl", "ax1", "al1", "ax2", "al2", "af"] + \
             ["lx%d" % k for k in range(4)] + ["ll%d" % k for k in range(4)]
A = AluOpType
F = ActivationFunctionType
PAR = {"cy": 1.04, "pe": 0.5, "gam": 1.56, "ov": 40.0, "oa": 60.0, "same": 60.0, "cross": 120.0, "net": [5000.0, 10000.0, 5000.0, 10000.0], "rc": 500.0}
CFG = {"relay": 1, "full": 1, "soon": 0.05, "eqw": [512, 512, 512], "inc": [0, 0, 0], "oh": 0, "xqv": [[], [3], [3]], "zcut": [[0, 64, 128]] * 3, "chunks": [[512, 512, 512, 512]] * 3, "wide": 3, "pen": 1000.0, "iters": 400, "seed": 3,
       "moves": 25000, "temp": 100.0, "mean": 0.2}
PLAN = {}
S0 = 12288.0


def pieces():
    xs = [(XO + 1024 * k, XO + 1024 * (k + 1)) for k in range(4)]
    lm = [(512 * k, 512 * (k + 1)) for k in range(4)]
    lm[3] = (lm[3][0], XO)
    return xs, lm


def nbits(m):
    return bin(m).count("1")


def routes(T, topo):
    n = len(T.cores); xs, lm = pieces(); out = {}

    def sides(r, dst):
        me = T.cores[r]; cs = sorted(topo.cores_of(me), key=lambda c: (topo.die(c) == topo.die(me), c == me))
        return [c for c in cs if topo.may_write(c, dst)], [c for c in cs if not topo.may_write(c, dst)]

    def put(c, sbuf, pc, wait, dst, dbuf, sem, mask=None):
        out.setdefault(c, []).append((sbuf, pc, wait, dst, dbuf, sem, topo.mask(c, dst) if mask is None else mask))

    late = []
    for r in range(n):
        me, d1, d2 = T.cores[r], T.cores[(r - 1) % n], T.cores[(r - 2) % n]
        P, O = sides(r, d1); home = topo.mask(me, P[0]) & ~topo.mask(me, d1)
        relay = CFG["relay"] and not topo.mates(topo.chip(me), topo.chip(d1)) and topo.mates(topo.chip(d1), topo.chip(d2))
        for k in range(3):
            put(me, "XB0", xs[k], None, P[k], "XB0", "hx", None if CFG["full"] else home)
            put(P[k], "XB0", xs[k], "hx", d1, "XB1", "ax1")
        put(me, "XB0", xs[3], None, d1, "XB1", "ax1")
        if relay:
            P2 = sides((r - 2) % n, d1)[0]
            for k in range(4):
                put(me, "XB0", lm[k], None, O[k], "XB0", "hl", home)
                put(O[k], "XB0", lm[k], "hl", P2[k], "XB2", "af")
                late.append((P2[k], "XB2", lm[k], "af", d1, "XB1", "al1"))
                if k < 3:
                    put(P[k], "XB0", xs[k], None, O[k], "XB0", "hx", home)
                    put(O[k], "XB0", xs[k], "hx", d2, "XB2", "ax2")
                    late.append((P2[k], "XB2", lm[k], None, d2, "XB2", "al2", home))
            late.append((me, "XB0", xs[3], None, d2, "XB2", "ax2"))
        else:
            for k in range(3):
                put(me, "XB0", lm[k], None, P[k], "XB0", "hl", home)
                put(P[k], "XB0", lm[k], "hl", d1, "XB1", "al1")
                put(P[k], "XB0", xs[k], None, d2, "XB2", "ax2")
                put(P[k], "XB0", lm[k], None, d2, "XB2", "al2")
            put(me, "XB0", lm[3], None, d1, "XB1", "al1")
            put(me, "XB0", lm[3], None, d2, "XB2", "af")
            put(me, "XB0", xs[3], None, d2, "XB2", "ax2")
    for w in sorted(late, key=lambda w: w[5] == "XB2"):
        put(*w)
    return out


def arrivals(R, core):
    got = {}
    for ws in R.values():
        for w in ws:
            if w[3] == core:
                got[w[5]] = got.get(w[5], 0) + nbits(w[6])
    return got


def helper_program(g, core, T, topo):
    R = routes(T, topo); got = arrivals(R, core); tot = 0
    for sbuf, (a, b), wait, dst, dbuf, sem, mask in R.get(core, []):
        if wait:
            g.wait_ge(T.sem[wait], got[wait])
        rid, pid, _ = topo.addr(dst)
        g.remote_dma(T[dbuf][:, a:b], T[sbuf][:, a:b], T.sem[sem], T.sem.sent, pid, rid, mask); tot += nbits(mask)
    if tot:
        g.wait_ge(T.sem.sent, tot)


def overlap(r, s):
    if r[0] != s[0] or r[2] <= s[1] or s[2] <= r[1]:
        return False
    if r[3] == s[3] and r[3] > 1 and (r[1] - s[1]) % r[3] != 0:
        return False
    return True


def build(T, topo, rank, place):
    ops = []
    nxt = {"bf": 0, "f32": 0, "f16": 0, "i32": 0, "u16": 0}
    CY, PE, GAM, OV, OA = PAR["cy"], PAR["pe"], PAR["gam"], PAR["ov"], PAR["oa"]
    temps = {}

    def new(buf, n):
        a = nxt[buf]; nxt[buf] = a + (n + 15) // 16 * 16
        return (buf, a, a + n, 1)

    def slot(n=128, whole=False):
        name = "ps_%d" % len(temps); temps[name] = 4 if whole or n > 128 else 1
        return (name, 0, n, 1)

    def sub(r, a, b, st=1):
        return (r[0], r[1] + a, r[1] + b, st)

    def ap(r):
        name, a, b = r[0], r[1], r[2]
        if name in temps:
            bank, c = place[name]; name = "ps%d" % bank; a += 128 * c; b += 128 * c
        return T[name][:, a:b:r[3]] if r[3] > 1 else T[name][:, a:b]

    def ln(r):
        return (r[2] - r[1] + r[3] - 1) // r[3]

    def two(*rs):
        return all(r[0] in ("bf", "f16", "u16", "XB0", "XB1", "XB2") for r in rs)

    def add(q, fn, rd, wr, cost, **kw):
        o = {"alt": {q: (fn, cost)}, "rd": [r for r in rd if isinstance(r, tuple)], "wr": wr, "lat": 0.0}
        o.update(kw); ops.append(o)

    def either(*makers):
        o = None
        for mk in makers:
            mk(); x = ops.pop()
            if o is None:
                o = x
            else:
                o["alt"].update(x["alt"]); o["rd"] = o["rd"] + x["rd"]
        ops.append(o)

    def row(name, k, q=None):
        ops[-1].setdefault("row", []).append((name, k))
        if q:
            ops[-1]["alt"] = {q: ops[-1]["alt"][q]}

    def val(x):
        return ap(x) if isinstance(x, tuple) else x

    def src(x):
        return ap(x[0]).indirect(ap(x[1])) if isinstance(x, list) else ap(x)

    def rds(x):
        return list(x) if isinstance(x, list) else [x]

    def vcost(out, x, per):
        return 50 + ln(out) * GAM * CY if isinstance(x, list) else OV + max(64, ln(out) * per) * CY

    def fast(out, x):
        return 0.5 if not isinstance(x, list) and two(out, x) else 1

    def cp(out, x):
        add("v", lambda q: q.tensor_copy(ap(out), src(x)), rds(x), [out], vcost(out, x, fast(out, x)))

    def ts(out, x, s1, o1, s2=None, o2=None):
        def fn(q):
            if o2 is None:
                return q.tensor_scalar(ap(out), src(x), val(s1), None, o1)
            return q.tensor_scalar(ap(out), src(x), val(s1), val(s2), o1, o2)
        add("v", fn, rds(x) + [s1, s2], [out], vcost(out, x, fast(out, x)))

    def tt(out, x, y, o):
        per = 1 if (not isinstance(x, list) and x[0] in temps) or y[0] in temps else 2
        add("v", lambda q: q.tensor_tensor(ap(out), src(x), ap(y), o), rds(x) + [y], [out], vcost(out, x, per))

    def act(out, x, f, bias=0.0, scale=1.0, extra=0.0):
        c = 65 + ln(out) * GAM * CY if isinstance(x, list) else OA + max(64, ln(out)) * CY
        add("a", lambda q: q.activation(ap(out), src(x), f, bias=val(bias), scale=val(scale)), rds(x) + [bias, scale], [out], c + extra)

    def lin(out, x, scale=1.0, bias=0.0):
        either(lambda: act(out, x, F.Identity, bias=bias, scale=scale),
               lambda: cp(out, x) if (scale, bias) == (1.0, 0.0) else ts(out, x, scale, A.mult, bias, A.add))

    def relu(out, x, bias=0.0, scale=1.0):
        either(lambda: act(out, x, F.Relu, bias=bias, scale=scale),
               lambda: ts(out, x, bias, A.add, 0.0, A.max) if scale == 1.0 else ts(out, x, scale, A.mult, 0.0, A.max))

    def pcost(l, r):
        return max(min(64, ln(l)), ln(r)) * (4 if l[0] == "f32" else 1)

    def mm(groups, first=True, last=True):
        def fn(q):
            ins = None
            for out, terms in groups:
                for n, (l, r) in enumerate(terms):
                    ins = q.matmul(ap(out), ap(l), ap(r), first and n == 0, last and n == len(terms) - 1)
            return ins
        rd = [x for _, terms in groups for t in terms for x in t]
        add("p", fn, rd, [o for o, _ in groups], 30 + PE * sum(pcost(l, r) for _, terms in groups for l, r in terms))

    def mm1(terms, n=128):
        p = slot(n); mm([(p, terms)])
        return p

    def dma(q, out, in_, rd, wr, sem, lat):
        add(q, lambda e: e.dma_start(out, in_), rd, wr, 50.0, sem=sem, inc=16, lat=lat)

    XB = [("XB%d" % t, 0, XW, 1) for t in range(3)]
    Ct = ("Ct", 0, M, 1); cqi = ("cqi", 0, M, 1); pti = ("pti", 0, 16, 1); thi = ("thi", 0, 2, 1); ypo = ("ypo", 0, 16, 1)
    Yc = ("Yc", 0, M, 1)
    xsp, lmp = pieces()

    def half(r, a):
        return sub(r, 128 * a, 128 * a + 128)

    dma("s", T.pti[:], T.pt[:], [], [pti], "lpt", 2000.0)
    dma("s", T.cqi[:], T.cq[:], [], [cqi], "lcq", 2300.0)
    dma("s", T.thi[0:8, 0:2], T.th[:], [], [thi], "lth", 2300.0)
    for k, (a, b) in enumerate(xsp):
        dma("s", T.XB0[:, a:b], T.xs[:, a - XO:b - XO], [], [sub(XB[0], a, b)], "lx%d" % k, 3200.0 + 900 * k)
    for k, (a, b) in enumerate(lmp):
        b = min(b, H)
        dma("s", T.XB0[:, a:b], T.lim[:, a:b], [], [sub(XB[0], a, b)], "ll%d" % k, 6300.0 + 450 * k)

    def iota(out, pat, base, cm):
        add("g", lambda q: q.iota(ap(out), pat, base, cm, allow_small_or_imprecise_dtypes=True), [], [out], 130 + 2 * ln(out) * CY)

    def asel(out, x, pat, o, base, cm, fill=0.0):
        add("g", lambda q: q.affine_select(ap(out), ap(x), pat, o, fill, base, cm), [x], [out], 170 + 2 * ln(out) * CY)

    def copy(out, x):
        either(lambda: lin(out, x), lambda: asel(out, x, [[0, ln(out)]], A.is_ge, 0, 0))

    MAGIC = 12582912.0
    cP, cH, c16, cI, cW, cS = [new("f32", 1) for _ in range(6)]
    xh = new("bf", 128); iob = new("bf", M); posT = new("bf", M); io16 = new("bf", 16)
    iota(cP, [[0, 1]], 0, 1)
    iota(xh, [[16, 8], [0, 16]], 0, 0)
    iota(io16, [[1, 16]], 0, 0)
    iota(sub(iob, 0, 144), [[1, 144]], 0, 0)
    iota(sub(iob, 144, M), [[1, M - 144]], 144, 0)
    iota(posT, [[1, 128], [128, 2]], 0, 0)
    eqk = new("f32", 16); t16 = new("f32", 16); t16b = new("f32", 16)
    ts(cH, cP, -7.5, A.add, 0.0625, A.mult)
    ts(c16, cH, MAGIC, A.add, MAGIC, A.subtract)
    lin(cH, c16, scale=16.0); c16 = cH
    tt(cI, cP, c16, A.subtract)
    (B, nB, G8, I, nI, nIbig, nI32, nI4032, nI127, nTri, Wr, M1, Bw, Bs, BD, I3232, I2080, I16k, I14k, nB2k, B8k, nIh, eps,
     zero) = [new("bf", 128) for _ in range(24)]
    B32 = new("f32", 128); Z = new("bf", 143); Zw = new("bf", 143); Sel = new("bf", 2048)
    io128 = sub(iob, 0, 128)
    add("v", lambda q: q.memset(ap(zero), 0.0), [], [zero], OV + 64 * CY, early=1)
    ts(B, xh, c16, A.is_equal)
    ts(eqk, io16, cI, A.is_equal)
    ts(Z, sub(iob, 0, 143), c16, A.subtract, 15.0, A.is_equal)
    ts(I, io128, cP, A.is_equal)
    for k in range(16):
        o = sub(Sel, 128 * k, 128 * k + 128)
        either(lambda: lin(o, B, scale=sub(eqk, k, k + 1)), lambda: asel(o, B, [[16, 8], [0, 16]], A.is_equal, k, -1))
    Sel0 = sub(Sel, 0, 128)
    ts(t16, io16, cI, A.is_lt, 1.0, A.add)
    add("v", lambda q: q.tensor_reduce(ap(cW), ap(t16), AxisListType.X, A.mult), [t16], [cW], 110.0)
    ts(t16b, io16, cI, A.is_gt, 1.0, A.add)
    add("v", lambda q: q.tensor_reduce(ap(cS), ap(t16b), AxisListType.X, A.mult), [t16b], [cS], 110.0)
    for o, x, s in ((Zw, Z, cW), (nB, B, -1.0), (nI, I, -1.0), (B32, B, 1.0), (nIbig, I, -65536.0),
                    (I2080, I, 2080.0 * 128), (I3232, I, 3232.0), (Bs, B, cS), (I14k, I, 14336.0), (nI32, I, -32.0), (nI4032, I, -4032.0),
                    (Bw, B, cW), (I16k, I, 16384.0), (nB2k, B, -2048.0), (B8k, B, 8192.0), (nIh, I, -0.5), (nI127, I, -127.5)):
        if x is I:
            either(lambda: lin(o, x, scale=s), lambda: asel(o, zero, [[1, 128]], A.not_equal, 0, -1, s))
        else:
            lin(o, x, scale=s)
    ts(G8, xh, 0.0625, A.mult, cP, A.is_equal)
    act(eps, zero, F.Exp, bias=-4.852030264, extra=1600.0); ops[-1]["early"] = 1
    asel(nTri, nB, [[1, 128]], A.is_gt, 0, -1)
    lin(Wr, mm1([(I, B), (nI32, nTri)]), scale=0.05)
    lin(M1, mm1([(I, I16k), (I, B8k)]))
    lin(BD, mm1([(Bs, I)]), scale=2.0 ** -16)
    Gw = [new("bf", M) for _ in range(3)]
    for a in (0, 1):
        copy(half(Gw[a], 1 - a), half(iob, 1 - a))
    lin(half(Gw[2], 1), half(iob, 1), scale=2.0, bias=-255.0)

    def W(j, z=Z):
        return sub(z, 15 - j, 143 - j)

    thb = new("bf", 16)
    add("v", lambda q: q.memset(ap(thb), 0.0), [], [thb], OV + 64 * CY)
    add("v", lambda q: q.tensor_copy(T.bf[0:8, thb[1]:thb[1] + 2], T.thi[0:8, 0:2]), [thi, thb], [thb], 110.0)
    p = mm1([(G8, thb)], 16)
    lin(sub(XB[0], TO, TO + 1), sub(p, 0, 1), scale=-1.0, bias=64.0)
    lin(sub(XB[0], TO + 1, XO), sub(p, 1, 16), bias=-127.0)

    ptu = new("u16", 16); Pn = new("bf", M)
    cp(ptu, pti)
    ts(half(Ct, 1), sub(cqi, 1, M, 2), S0, A.add)
    lin(Pn, [posT, ptu])
    L = [new("u16", 16) for _ in range(3)]; PS = [new("bf", M) for _ in range(4)]
    p = slot(16)
    mm([(sub(p, 8 * a, 8 * a + 8), [(W(i), sub(Pn, 2 * i + a, M, 32)) for i in range(16)]) for a in (0, 1)])
    ts(L[0], p, 0.0625, A.mult)
    for a in (0, 1):
        copy(half(PS[0], a), sub(Pn, a, M, 2))

    Dn = new("f16", M); En = new("bf", M); upn = new("f32", M)
    ts(Dn, cqi, -2048.0, A.add)
    ts(En, Dn, 2047.0, A.is_equal, 2.0 ** -6, A.mult)
    ts(upn, [cqi, ptu], NO - 0.5, A.min, -2048.0, A.add)

    def bits(out, x, p):
        rn = new("f32", 128)
        mm([(p, [(BD, x), (BD, eps)])])
        ts(rn, p, MAGIC, A.add, MAGIC, A.subtract)
        tt(out, p, rn, A.is_lt)

    def relation(n, Lst, old=None):
        a = n & 1
        R = {k: new("bf", 128) for k in ("E", "Pm", "inC")}
        eqb = new("bf", 2048); La = sub(Lst, 8 * a, 8 * a + 8); w = CFG["eqw"][n]
        upr = new("f32", w)
        if old is None:
            R["Dm"] = sub(Dn, a, M, 2); R["E"] = sub(En, a, M, 2)
            if w > 128:
                copy(sub(upr, 0, 128), sub(upn, a, M, 2))
            else:
                upr = sub(upn, a, M, 2)
        else:
            R["Dm"] = new("f16", 128)
            ts(R["Dm"], half(Ct, a), S0 + NO, A.min, -S0 - 2048, A.add)
            ts(R["E"], R["Dm"], 2047.0, A.is_equal, 2.0 ** -6, A.mult)
            ts(sub(upr, 0, 128), [Ct, La], S0 + NO - 0.5, A.min, -S0 - 2048, A.add)
        u = 128
        while u < w:
            copy(sub(upr, u, 2 * u), sub(upr, 0, u)); u *= 2
        Pk = slot(128, True); Ic = slot()
        for c in range(4):
            bc = slot(512); eq = sub(eqb, 512 * c, 512 * c + 512)
            mm([(half(bc, u), [(half(Sel, 4 * c + u), R["Dm"])]) for u in range(4)])
            for u in range(0, 512, w):
                tt(sub(eq, u, u + w), sub(bc, u, u + w), upr, A.is_equal); row("eq", 2048 * n + 512 * c + u)
            terms = [(W(4 * c + u, Zw), half(eq, u)) for u in range(4)]
            mm([(Pk, ([(I, R["E"])] if c == 0 and old is None else []) + terms)], first=c == 0, last=c == 3)
        if old is None:
            R["out"] = new("bf", 128); R["xB"] = new("f16", 128); R["yl"] = new("u16", 16); R["inT"] = new("bf", 128)
            FC = new("f32", 128); r16 = new("bf", 128)
            either(lambda: act(R["out"], Pk, F.Relu, bias=4096.0, scale=-262144.0), lambda: ts(R["out"], Pk, 0.0, A.is_equal, 4096.0, A.mult))
            relu(FC, mm1([(nI, R["Dm"]), (nTri, R["out"]), (I, R["out"])]), -2048.0)
            relu(r16, mm1([(I, io128), (nB, R["out"])]), scale=16.0)
            ts(R["xB"], mm1([(nI, r16), (B32, FC)]), -1.0, A.mult, 2048.0, A.add)
            ts(R["yl"], mm1([(W(i), sub(R["xB"], i // 2, 128, 8)) for i in range(16)], 16), 0.0625, A.mult, 2048.0, A.add)
        else:
            for k in ("out", "xB", "yl", "inT"):
                R[k] = old[k]
        lin(R["Pm"], Pk, bias=2.0 ** -9)
        if CFG["inc"][n]:
            mm([(Ic, [(I, half(eqb, k)) for k in range(16)])])
            lin(R["inC"], Ic)
        else:
            bits(R["inC"], R["Pm"], Ic)
        if old is None:
            lin(R["inT"], mm1([(R["inC"], I)]))
        return R

    def acting(R, t):
        a = t & 1
        for k in ("nact", "gone", "fe"):
            R[k] = new("bf", 128)
        R["capA"] = new("f32", 128); gd = new("bf", 128)
        ts(R["nact"], half(PS[t], a), 127.5, A.is_gt if a else A.is_lt, -32.0, A.mult)
        relu(R["gone"], mm1([(I, R["nact"]), (nB, R["out"])]), 1.0)
        tt(gd, mm1([(I, half(PS[t], a)), (nI, half(iob, a))]), R["gone"], A.mult)
        if t < 2:
            lin(half(Gw[t], a), mm1([(I, gd), (I, half(iob, a))]))
        else:
            lin(half(Gw[t], a), mm1([(I, gd), (I, half(iob, a)), (nI127, R["gone"])]), scale=2.0)
        lin(PS[t + 1], [Gw[t], L[t]])
        if t < 2:
            ts(L[t + 1], mm1([(W(i), sub(PS[t + 1], i, M, 16)) for i in range(16)], 16), 0.0625, A.mult)
        else:
            lin(ypo, mm1([(W(i), sub(PS[3], (i & 1) * 128 + (i >> 1), (i & 1) * 128 + 128, 8)) for i in range(16)], 16), scale=0.0625)
            dma("s", T.yp[:], T.ypo[:], [ypo], [], "op", 2000.0)

    def rooms(R):
        relu(R["fe"], mm1([(I, R["E"]), (nTri, R["E"]), (nI, R["gone"])]), scale=64.0)
        lin(R["capA"], mm1([(I, R["Dm"]), (nIbig, R["fe"]), (nIbig, R["gone"])]), bias=S0 + 2048)

    def onehots():
        paT = new("f32", 16); OH = new("bf", 16 * M)
        p = slot(16)
        mm([(sub(p, 8 * ch, 8 * ch + 8), [(half(PS[0], ch), sub(I, 0, 128, 16))]) for ch in (0, 1)])
        lin(paT, p)
        for u in range(16):
            if CFG["oh"]:
                for a in (0, 1):
                    ts(half(OH, 2 * u + a), half(iob, a), sub(paT, u, u + 1), A.is_equal); row("oh%d" % a, u)
            else:
                ts(sub(OH, M * u, M * u + M), iob, sub(paT, u, u + 1), A.is_equal); row("oh", u)
        return lambda ch, gr, a: half(OH, 2 * (8 * ch + gr) + a)

    def leaving(R, t, oh, marks):
        a = t & 1
        kb = new("bf", 128); Pc = new("bf", 128); rn = new("f32", 128); R["can"] = new("bf", 128); R["sg"] = new("bf", 128)
        p = slot()
        mm([(sub(p, 16 * gr, 16 * gr + 16), [(oh(ch, gr, a), sub(marks[ch], 16 * gr, 16 * gr + 16)) for ch in (0, 1)]) for gr in range(8)])
        lin(kb, p)
        relu(Pc, mm1([(kb, nIbig), (I, R["Pm"])]))
        bits(R["can"], Pc, slot())
        act(R["sg"], mm1([(I, R["can"]), (nI, R["gone"])]), F.Sign, bias=0.5, scale=-1.0)

    Qu = new("u16", 128); hu = new("u16", 128); Qh = new("f16", 128); wq = new("f16", 128)
    yv, pp, cap, fin = [new("f32", 128) for _ in range(4)]; uu0 = new("bf", 128); pen = new("bf", 128)
    nI_ = new("i32", 128); hI = new("i32", 128)
    Xy = new("bf", 256); Cmp = new("bf", 2048); ad = new("f32", 2048)
    preJ, tw, ws, keep, eqL = [new("bf", 128) for _ in range(5)]
    odd = [None, new("i32", 1), new("i32", 1)]

    def front(R, t, Lst):
        a = t & 1; La = sub(Lst, 8 * a, 8 * a + 8); xw = sub(XB[t], XO, QO); lw = sub(XB[t], 0, H); XQ = sub(XB[t], QO, XW)
        if t == 0:
            ts(Qu, sub(upn, 0, M, 2), 2048.25, A.add)
        else:
            ts(Qu, [Ct, La], S0 + NO, A.min, -S0, A.add)
        ts(Qh, Qu, -2048.0, A.add)
        tt(yv, mm1([(Sel0, Qh), (B, R["out"])]), R["xB"], A.min)
        q32 = mm1([(I, Qh), (I2080, eps)])
        tt(pp, q32, yv, A.mult)
        tt(nI_, mm1([(I3232, Qh)]), pp, A.add)
        ts(hI, nI_, 5, A.arith_shift_right, H - 1, A.bitwise_and)
        cp(hu, hI)
        tt(cap, mm1([(I, Qh), (I14k, R["gone"])]), R["capA"], A.max)
        c0 = 0
        for m, w in enumerate(CFG["chunks"][t]):
            c1 = c0 + w; xy = sub(Xy, c0 // 8, c1 // 8); xq = sub(XQ, c0, c1); d = slot(w, True)
            lin(xq, [xw, sub(Qu, c0 // 16, c1 // 16)])
            if m not in CFG["xqv"][t]:
                row("s%d" % t, 2 * m - 2.5, "a")
            else:
                row("v%d" % t, -1, "v")
            lin(xy, [sub(XB[t], XO, QO + c1), sub(R["yl"], c0 // 128, c1 // 128)])

            def fn(q, d=d, xq=xq, xy=xy, w=w):
                q.matmul(ap(d), ap(I), ap(xq), True, False)
                for u in range(8):
                    ins = q.matmul(ap(sub(d, u, w, 8)), ap(nI), ap(xy), False, u == 7)
                return ins
            add("p", fn, [I, nI, xq, xy], [d], 30 + PE * (w + 8 * max(64, w // 8)))
            act(sub(ad, c0, c1), d, F.Abs); row("s%d" % t, 2 * m)
            tt(sub(Cmp, c0, c1), [lw, sub(hu, c0 // 16, c1 // 16)], sub(ad, c0, c1), A.is_ge); row("v%d" % t, m)
            c0 = c1

    def decide(R, t):
        a = t & 1
        c1 = new("f32", 1); th1 = sub(XB[t], TO, TO + 1); th2 = sub(XB[t], TO + 1, TO + 2)
        if t == 0:
            lin(c1, th1)
        else:
            ts(c1, odd[t], -1.0, A.mult, th1, A.add)
        ts(preJ, mm1([(B8k, R["fe"]), (nIbig, R["inC"]), (nI, Qh)]), 6145.5, A.is_gt, c1, A.mult)
        z = slot(128, True)
        mm([(z, [(nI4032, eps), (I, R["nact"]), (nI32, R["gone"]), (nI32, R["gone"])])], last=False)
        cuts = CFG["zcut"][t]
        for m0, m1 in zip(cuts, cuts[1:]):
            if m1 == 128:
                mm([(z, [(nI32, R["sg"]), (I, preJ)])], first=False, last=False)
            mm([(sub(z, m0, m1), [(W(j), sub(Cmp, 16 * m0 + j, 16 * m1, 16)) for j in range(16)])], first=False, last=m1 == 128)
        tt(uu0, z, R["sg"], A.mult)
        either(lambda: act(pen, z, F.Relu, scale=-128.0), lambda: ts(pen, z, 0.0, A.min, -128.0, A.mult))
        act(tw, mm1([(I, uu0), (nI, pen)]), F.Exp, bias=22.8, scale=3.4657359)
        either(lambda: act(keep, z, F.Relu, bias=th2, scale=-1.0), lambda: ts(keep, z, th2, A.is_lt))
        tt(ws, mm1([(Wr, tw)]), tw, A.is_lt)
        tt(wq, mm1([(I, Qh)]), ws, A.mult)
        tt(eqL, mm1([(Bw, ws)]), R["Pm"], A.is_equal)
        v = slot(128, True)
        mm([(v, [(I16k, R["fe"]), (I16k, R["gone"]), (nIbig, keep), (nB2k, ws)])], last=False)
        mm([(v, [(B, wq)])], first=False, last=False)
        mm([(v, [(M1, eqL)])], first=False)
        if t == 2:
            tt(fin, v, cap, A.max)
            ts(sub(Yc, a, M, 2), fin, S0 + NO, A.min, -S0, A.add)
            return None
        tt(half(Ct, a), v, cap, A.max)
        cT = new("bf", 128); jb = new("bf", 1); oI = new("i32", 1); e1 = sub(eps, 0, 1)
        act(cT, mm1([(R["inC"], I), (ws, nI), (R["can"], nI), (R["sg"], nIh), (keep, I)]), F.Abs, bias=0.5)
        lin(jb, mm1([(ws, e1), (eqL, e1)], 1), scale=16384.0)
        cp(oI, mm1([(eps, jb)], 1)); ts(odd[t + 1], oI, 1, A.bitwise_and)
        return cT

    RT = routes(T, topo); got = arrivals(RT, T.cores[rank]); net = PAR["net"]

    def send(k, sbuf, pc, wait, dst, dbuf, sem, mask):
        rid, pid, _ = topo.addr(dst); a, b = pc
        add("g", lambda q: q.remote_dma(T[dbuf][:, a:b], T[sbuf][:, a:b], T.sem[sem], T.sem.sent, pid, rid, mask),
            [(sbuf, a, b, 1)], [("net", k, k + 1, 1)], PAR["rc"], remote=nbits(mask))
        row("net", k)

    def arrive(sem, s, a, b, k, lat):
        add("x", None, [("net", 0, k, 1)], [sub(XB[s], a, b)], 0.0, sem=sem, inc=got[sem], lat=lat)
    for k, w in enumerate(RT[T.cores[rank]]):
        if k == 8:
            arrive("af", 2, lmp[3][0], XO, 8, net[0])
        send(k, *w)
    arrive("ax1", 1, XO, QO, 4, net[1]); arrive("al1", 1, 0, XO, 9, net[2])
    arrive("ax2", 2, XO, QO, 10, net[3]); arrive("al2", 2, 0, lmp[3][0], 10, net[3])

    R0 = relation(0, L[0])
    acting(R0, 0); rooms(R0)
    R1 = relation(1, L[0])
    oh = onehots()
    leaving(R0, 0, oh, [R0["inT"], R1["inT"]])
    acting(R1, 1); rooms(R1)
    front(R0, 0, L[0])
    cT0 = decide(R0, 0)
    leaving(R1, 1, oh, [cT0, R1["inT"]])
    R2 = relation(2, L[1], R0)
    acting(R2, 2); rooms(R2)
    front(R1, 1, L[0])
    cT1 = decide(R1, 1)
    ts(sub(Yc, 1, M, 2), half(Ct, 1), S0 + NO, A.min, -S0, A.add)
    leaving(R2, 2, oh, [R0["inT"], cT1])
    front(R2, 2, L[1])
    decide(R2, 2)
    dma("s", T.yc[:], T.Yc[:], [Yc], [], "oc", 2500.0)
    for k in nxt:
        assert nxt[k] <= SCRATCH[k][1][1], (k, nxt[k])
    return ops, temps


def graph(ops, temps):
    n = len(ops); deps = []; byname = {}
    for i, o in enumerate(ops):
        d = set()
        for r in o["rd"] + o["wr"]:
            for j, w, s in byname.get(r[0], []):
                if w and overlap(r, s):
                    d.add(j)
        for r in o["wr"]:
            for j, w, s in byname.get(r[0], []):
                if overlap(r, s):
                    d.add(j)
        deps.append(d)
        for r in o["rd"]:
            byname.setdefault(r[0], []).append((i, False, r))
        for r in o["wr"]:
            byname.setdefault(r[0], []).append((i, True, r))
    succ = [[] for _ in range(n)]
    for i in range(n):
        for j in deps[i]:
            succ[j].append(i)
    tmp = [sorted(set(r[0] for r in o["rd"] + o["wr"] if r[0] in temps)) for o in ops]
    users = {t: [i for i in range(n) if t in tmp[i]] for t in temps}
    return deps, succ, tmp, users


def insert_schedule(ops, pred, succ, key, pen, back):
    n = len(ops); same, cross = PAR["same"], PAR["cross"]
    busy = {q: [] for q in "vapgsx"}; st = [0.0] * n; en = [0.0] * n; eng = [None] * n
    left = [len(d) for d in pred]; ready = [i for i in range(n) if left[i] == 0]
    while ready:
        i = min(ready, key=lambda j: key[j]); ready.remove(i); best = None; o = ops[i]
        for q in o["alt"]:
            c = o["alt"][q][1]; t = o["lat"] if back and not pred[i] else 0.0
            for j in pred[i]:
                u = en[j] + (o["lat"] if back else ops[j]["lat"]) + (cross if eng[j] != q else 0.0 if q == "p" else same)
                if u > t:
                    t = u
            for a, b in busy[q]:
                if b <= t:
                    continue
                if a >= t + c:
                    break
                t = b
            v = t + c + (pen[i] if q == "v" and len(o["alt"]) > 1 else 0.0)
            if best is None or v < best[0]:
                best = (v, q, t, c)
        _, q, t, c = best
        eng[i] = q; st[i] = t; en[i] = t + c; busy[q].append((t, t + c)); busy[q].sort()
        for k in succ[i]:
            left[k] -= 1
            if left[k] == 0:
                ready.append(k)
    return st, en, eng


def late_psum(ops, succ, st, en, eng):
    row = sorted((i for i in range(len(ops)) if eng[i] == "p"), key=lambda i: -st[i]); placed = []
    for i in row:
        c = en[i] - st[i]
        t = min([st[k] - (0.0 if eng[k] == "p" else PAR["cross"]) for k in succ[i]]) - c
        for a, b in placed:
            if a >= t + c:
                continue
            if b <= t:
                break
            t = a - c
        if t > st[i]:
            st[i] = t; en[i] = t + c
        placed.append((st[i], en[i])); placed.sort(reverse=True)


def realize(ops, temps, G, st, eng):
    deps0, succ, tmp, users = G
    n = len(ops); same, cross = PAR["same"], PAR["cross"]
    for kind in ([i for i in range(n) if "remote" in ops[i]], [i for i in range(n) if eng[i] == "s" and not ops[i]["rd"]]):
        for i, t in zip(kind, sorted(st[j] for j in kind)):
            st[i] = t
    seq = {q: sorted((i for i in range(n) if eng[i] == q), key=lambda i: (st[i], i)) for q in "vapgsx"}
    deps = [set(d) for d in deps0]; end = [0.0] * n; start = [0.0] * n; left = [len(d) for d in deps0]; rt = [0.0] * n
    free = dict.fromkeys(seq, 0.0); bank_by = [None] * 8; place = {}; order = []
    tenant = [[None] * 4 for _ in range(8)]; todo = {t: len(users[t]) for t in temps}; gone_t = {}
    while len(order) < n:
        pick = None
        for q in seq:
            for i in seq[q][:8]:
                if left[i]:
                    break
                t = max(free[q], rt[i]); where = None; ok = True
                for x in tmp[i]:
                    if x in place:
                        u = bank_by[place[x][0]]
                        if eng[u] != q and end[u] + cross > t:
                            t = end[u] + cross
                        continue
                    best = None
                    for b in range(8):
                        u = bank_by[b]; tb = t if u is None or eng[u] == q else max(t, end[u] + cross)
                        row = tenant[b]; live = sum(y is not None and todo[y] > 0 for y in row)
                        if temps[x] == 4:
                            if live:
                                continue
                            c = max([tb] + [gone_t[y] + cross for y in row if y is not None]); c = (c, b, 0, c)
                        else:
                            if live == 4 or b < CFG["wide"]:
                                continue
                            c = min((tb if y is None else max(tb, gone_t[y] + cross), s) for s, y in enumerate(row) if y is None or todo[y] == 0)
                            c = (c[0] + 60 * live, b, c[1], c[0])
                        if best is None or c[0] < best[0]:
                            best = c
                    if best is None:
                        ok = False
                        break
                    t = best[3]; where = (x, best[1], best[2])
                if ok:
                    if pick is None or (t, st[i]) < pick[0]:
                        pick = ((t, st[i]), i, where)
                    break
        if pick is None:
            return None
        (t, _), i, where = pick; q = eng[i]
        start[i] = t; end[i] = t + ops[i]["alt"][q][1]; free[q] = end[i]; seq[q].remove(i); order.append(i)
        if where:
            x, b, s = where; place[x] = (b, s)
            for c in range(s, s + temps[x]):
                if tenant[b][c] is not None:
                    deps[i].update(users[tenant[b][c]])
                tenant[b][c] = x
        for x in tmp[i]:
            b = place[x][0]; u = bank_by[b]
            if u is not None and u != i and eng[u] != q:
                deps[i].add(u)
            bank_by[b] = i; todo[x] -= 1
            gone_t[x] = max(gone_t.get(x, 0.0), end[i])
        for k in succ[i]:
            rt[k] = max(rt[k], end[i] + ops[i]["lat"] + (cross if eng[k] != q else 0.0 if q == "p" else same)); left[k] -= 1
    return max(end[i] + ops[i]["lat"] for i in range(n)), order, deps, place, start, eng


def search(ops, temps, iters, seed):
    G = graph(ops, temps); deps, succ = G[0], G[1]; n = len(ops); x = [seed]

    def rnd(k):
        x[0] = (x[0] * 1103515245 + 12345) % 2147483648
        return (x[0] >> 8) % k
    flex = [i for i in range(n) if len(ops[i]["alt"]) > 1]
    tail = [0.0] * n
    for i in range(n - 1, -1, -1):
        tail[i] = min(a[1] for a in ops[i]["alt"].values()) + ops[i]["lat"] + max([PAR["cross"] + tail[k] for k in succ[i]] + [0.0])
    key = [-t for t in tail]; pen = [CFG["pen"]] * n; best = None; cur = None
    early = [i for i in range(n) if ops[i].get("early")]
    for it in range(iters):
        k2 = list(key); p2 = list(pen)
        if it:
            for _ in range(rnd(12)):
                k2[rnd(n)] += (rnd(41) - 20) * 100.0
            for _ in range(rnd(5)):
                p2[flex[rnd(len(flex))]] = [5000.0, 2000.0, 1000.0, 500.0, 200.0, 0.0][rnd(6)]
        for i in early:
            k2[i] = -1e9
        st, en, eng = insert_schedule(ops, deps, succ, k2, p2, False)
        if it % 4 == 0:
            sb, eb, _ = insert_schedule(ops, succ, deps, [-(en[i] + ops[i]["lat"]) for i in range(n)], p2, True)
            k2 = [-e for e in eb]
            for i in early:
                k2[i] = -1e9
            st, en, eng = insert_schedule(ops, deps, succ, k2, p2, False)
        if cur is not None and max(en[i] + ops[i]["lat"] for i in range(n)) > cur + 400:
            continue
        late_psum(ops, succ, st, en, eng)
        r = realize(ops, temps, G, st, eng)
        if r is not None and (cur is None or r[0] <= cur + 300.0 * (1 - it / iters) * rnd(100) / 100):
            cur = r[0]; key, pen = k2, p2
            if best is None or r[0] < best[0]:
                best = r
    return best


def anneal(ops, temps, order, eng, iters, seed):
    deps, succ, tmp, users = graph(ops, temps); n = len(ops); same, cross = PAR["same"], PAR["cross"]
    before = [set(d) for d in deps]; after = [set(s) for s in succ]
    for kind in ([i for i in range(n) if "remote" in ops[i]], [i for i in range(n) if "s" in ops[i]["alt"] and not ops[i]["rd"]]):
        for i, j in zip(kind, kind[1:]):
            before[j].add(i); after[i].add(j)
    pre = [[(j, ops[j]["lat"]) for j in d] for d in deps]; cost = [{q: a[1] for q, a in o["alt"].items()} for o in ops]
    lat = [o["lat"] for o in ops]; nuse = {t: len(users[t]) for t in temps}; x = [seed]; wide = CFG["wide"]
    rem = [i for i in range(n) if "remote" in ops[i]]

    def rnd(k):
        x[0] = (x[0] * 1103515245 + 12345) % 2147483648
        return (x[0] >> 8) % k

    def run(lst, eng, full=False):
        end = [0.0] * n; crit = [-1] * n; free = dict.fromkeys("vapgsx", 0.0); last = dict.fromkeys("vapgsx", -1)
        by = [-1] * 8; live = [0] * 8; tenant = [[None] * 4 for _ in range(8)]; todo = dict(nuse); gone = {}; place = {}
        more = [set() for _ in range(n)] if full else None
        for i in lst:
            q = eng[i]; t = free[q]; c = last[q]; sq = 0.0 if q == "p" else same
            for j, l in pre[i]:
                u = end[j] + l + (cross if eng[j] != q else sq)
                if u > t:
                    t = u; c = j
            for y in tmp[i]:
                if y in place:
                    b = place[y][0]; j = by[b]
                    if eng[j] != q and end[j] + cross > t:
                        t = end[j] + cross; c = j
                else:
                    best = None; whole = temps[y] == 4
                    for b in range(8):
                        k = live[b]
                        if (k > 0) if whole else (k == 4 or b < wide):
                            continue
                        j = by[b]; u = t; s = 0
                        if j >= 0 and eng[j] != q and end[j] + cross > u:
                            u = end[j] + cross
                        row = tenant[b]
                        if whole:
                            for w in row:
                                if w is not None and gone[w] > u:
                                    u = gone[w]
                        else:
                            m = None
                            for s2 in range(4):
                                w = row[s2]
                                if w is None or todo[w] == 0:
                                    g2 = 0.0 if w is None else gone[w]
                                    if m is None or g2 < m:
                                        m = g2; s = s2
                            if m > u:
                                u = m
                        if best is None or u + 60 * k < best[0]:
                            best = (u + 60 * k, u, b, s)
                    if best is None:
                        return None
                    _, u, b, s = best
                    if u > t:
                        t = u; c = by[b]
                    place[y] = (b, s); row = tenant[b]
                    for s2 in range(s, s + temps[y]):
                        if full and row[s2] is not None:
                            more[i].update(users[row[s2]])
                        row[s2] = y
                    live[b] += temps[y]
                if full and by[b] >= 0 and eng[by[b]] != q:
                    more[i].add(by[b])
            e = t + cost[i][q]; end[i] = e; crit[i] = c; free[q] = e; last[q] = i
            for y in tmp[i]:
                b = place[y][0]; by[b] = i; todo[y] -= 1; gone[y] = max(gone.get(y, 0.0), e + cross)
                if todo[y] == 0:
                    live[b] -= temps[y]
        top = max(range(n), key=lambda i: end[i] + lat[i]); span = end[top] + lat[top]
        if full:
            return span, lst, [deps[i] | more[i] for i in range(n)], place, [end[i] - cost[i][eng[i]] for i in range(n)], eng
        path = []
        while top >= 0:
            path.append(top); top = crit[top]
        span += CFG["soon"] * sum(end[i] for i in rem)
        return span + CFG["mean"] * sum(end) / n, path, span, end

    lst = list(order); eng = list(eng); cur = run(lst, eng)
    if cur is None:
        return None
    best = (cur[2], lst, eng)
    for it in range(iters):
        i = cur[1][rnd(len(cur[1]))] if rnd(10) < 6 else rnd(n)
        l2 = lst; e2 = eng; kind = rnd(10)
        if kind < 2 and len(cost[i]) > 1:
            e2 = list(eng); qs = [q for q in cost[i] if q != eng[i]]; e2[i] = qs[rnd(len(qs))]
        if kind >= 1:
            p = lst.index(i); hops = 1 + rnd(5) * rnd(5) * rnd(2); step = -1 if rnd(10) < 6 else 1; r = p; q = e2[i]
            while hops and 0 <= r + step < n:
                r += step
                if e2[lst[r]] == q:
                    hops -= 1
            rel = before if step < 0 else after
            seg = lst[r:p] if step < 0 else lst[p + 1:r + 1]
            pull = set(rel[i]); go = []; stay = []
            for j in (reversed(seg) if step < 0 else seg):
                if j in pull:
                    go.append(j); pull |= rel[j]
                else:
                    stay.append(j)
            if step < 0:
                l2 = lst[:r] + go[::-1] + [i] + stay[::-1] + lst[p + 1:]
            else:
                l2 = lst[:p] + stay + [i] + go + lst[r + 1:]
        new = run(l2, e2)
        if new is not None and new[0] <= cur[0] + CFG["temp"] * (1 - it / iters) * rnd(100) / 100:
            cur = new; lst = l2; eng = e2
            if new[2] < best[0]:
                best = (new[2], lst, eng)
        if it % 16 == 0:
            end = cur[3]; l2 = sorted(lst, key=lambda j: end[j] - cost[j][eng[j]]); new = run(l2, eng)
            if new is not None and new[0] <= cur[0] + 20:
                cur = new; lst = l2
    return run(best[1], best[2], True)


def make_plan(ops, temps):
    deps, succ, _, _ = graph(ops, temps); n = len(ops); rows = {}
    pred = [set(d) for d in deps]; nxt = [list(s) for s in succ]
    for i, o in enumerate(ops):
        for name, k in o.get("row", ()):
            rows.setdefault(name, []).append((k, i))
    for row in rows.values():
        row.sort()
        for (_, i), (_, j) in zip(row, row[1:]):
            pred[j].add(i); nxt[i].append(j)
    tail = {}

    def far(i):
        if i not in tail:
            tail[i] = min(a[1] for a in ops[i]["alt"].values()) + ops[i]["lat"] + max([PAR["cross"] + far(k) for k in nxt[i]] + [0.0])
        return tail[i]
    for i in range(n - 1, -1, -1):
        far(i)
    key = [-1e9 if ops[i].get("early") else -tail[i] for i in range(n)]
    best = search(ops, temps, CFG["iters"], CFG["seed"])
    for pen in (200.0, 500.0, 1000.0, 2000.0):
        st, en, eng = insert_schedule(ops, pred, nxt, key, [pen] * n, False)
        late_psum(ops, nxt, st, en, eng)
        left = [len(d) for d in pred]; ready = [i for i in range(n) if not left[i]]; order = []
        while ready:
            i = min(ready, key=lambda j: (st[j], j)); ready.remove(i); order.append(i)
            for k in nxt[i]:
                left[k] -= 1
                if left[k] == 0:
                    ready.append(k)
        r = anneal(ops, temps, order, eng, 0, 1)
        if r is not None and (best is None or r[0] < best[0]):
            best = r
    return anneal(ops, temps, best[1], best[5], CFG["moves"], CFG["seed"])


def rank_program(g, core, T, topo):
    rank = T.rank_of(core)
    if rank is None:
        helper_program(g, core, T, topo)
        return
    place = {}
    ops, temps = build(T, topo, rank, place)
    if not PLAN:
        RT = routes(T, topo); r = max(range(len(T.cores)), key=lambda r: sum(w[2] is not None for w in RT[T.cores[r]]))
        PLAN["x"] = make_plan(*build(T, topo, r, {}))
    _, order, deps, pl, _s, eng = PLAN["x"]
    own = graph(ops, temps)[0]
    deps = [own[i] if "remote" in ops[i] else deps[i] for i in range(len(ops))]
    place.update(pl)
    queue = {"v": g.vector, "a": g.scalar, "p": g.tensor, "g": g, "s": g.sync}
    semof = {"v": "sv", "a": "sa", "p": "sp", "g": "sg"}
    pos = {i: k for k, i in enumerate(order)}
    need = set(); waits = {}
    for i in order:
        best = {}
        for j in deps[i]:
            if "sem" in ops[j] or eng[j] == "p" and eng[i] == "p":
                continue
            if eng[j] not in best or pos[j] > pos[best[eng[j]]]:
                best[eng[j]] = j
        waits[i] = list(best.values()) + sorted(j for j in deps[i] if "sem" in ops[j])
        need.update(best.values())
    count = {}; waited = {}; sent = 0; tok = {}
    for i in order:
        o = ops[i]; q = eng[i]
        if q == "x":
            tok[i] = (o["sem"], o["inc"]); count[o["sem"]] = o["inc"]
            continue
        for j in waits[i]:
            s, c = tok[j]
            if waited.get((q, s), 0) < c:
                queue[q].wait_ge(T.sem[s], c); waited[(q, s)] = c
        ins = o["alt"][q][0](queue[q])
        if "remote" in o:
            sent += o["remote"]
        elif "sem" in o:
            ins.then_inc(T.sem[o["sem"]], 16); tok[i] = (o["sem"], 16); count[o["sem"]] = 16
        elif i in need:
            s = semof[q]; count[s] = count.get(s, 0) + 1
            ins.then_inc(T.sem[s], 1); tok[i] = (s, count[s])
    g.wait_ge(T.sem.sent, sent)
    for s in count:
        if max([c for (q, s2), c in waited.items() if s2 == s] + [0]) < count[s]:
            g.sync.wait_ge(T.sem[s], count[s])
